import numpy as np
import ml_dtypes


def mxq(x, axis, fmt="e4m3"):
    dtype, down = {"e4m3": (ml_dtypes.float8_e4m3fn, 7), "e5m2": (ml_dtypes.float8_e5m2, 14)}[fmt]
    v = np.moveaxis(np.asarray(x, np.float32).astype(ml_dtypes.bfloat16).astype(np.float64), axis, -1)
    blocks = v.reshape(v.shape[:-1] + (-1, 32))
    amax = np.abs(blocks).max(-1, keepdims=True)
    byte = np.maximum(np.where(amax > 0, np.frexp(amax)[1] - 1 + 127, 0) - down, 1)
    scale = np.exp2(byte - 127.0)
    codes = (blocks / scale).astype(np.float32).astype(dtype).astype(np.float64)
    return np.moveaxis((codes * scale).reshape(v.shape), -1, axis)


WIDE = False


def mx_kscale(k):
    if not WIDE:
        return np.ones(k)
    levels = np.array([10, -10, 5, -5, 0])
    if k % 512:
        return np.exp2(np.random.permutation(np.resize(levels, k // 32))).repeat(32)
    a = np.empty((k // 512, 16))
    for p in range(k // 512):
        a[p, :8] = np.random.permutation(np.resize(levels, 8))
        for g in range(8):
            far = levels[np.abs(levels - a[p, g]) >= 10]
            a[p, g + 8] = far[np.random.randint(len(far))]
    return np.exp2(a.ravel()).repeat(32)


BF16 = ml_dtypes.bfloat16


def bf(x):
    return np.asarray(x, np.float32).astype(BF16)


def f64(x):
    return np.asarray(x).astype(np.float64)


E2M1 = np.array([0.0, 0.5, 1.0, 1.5, 2.0, 3.0, 4.0, 6.0, -0.0, -0.5, -1.0, -1.5, -2.0, -3.0, -4.0, -6.0])


def pack_weight(w, fmt):
    k, n = w.shape
    w = f64(bf(w)).reshape(k // 32, 32, n)
    amax = np.abs(w).max(1)
    if fmt == "e4m3":
        byte = np.frexp(amax)[1] - 1 + 127 - 7
    else:
        mant, ex = np.frexp(amax / 6.0)
        byte = np.where(mant > 0.5, ex, ex - 1) + 127
    byte = np.clip(np.where(amax > 0, byte, 1), 1, 254)
    scaled = (w * np.exp2(127.0 - byte)[:, None, :]).reshape(k, n).astype(np.float32)
    by_word = np.ascontiguousarray(scaled.reshape(k // 512, 128, 4, n).transpose(0, 1, 3, 2))
    if fmt == "e4m3":
        words = by_word.astype(ml_dtypes.float8_e4m3fn).view(np.uint8)
    else:
        c = by_word.astype(ml_dtypes.float4_e2m1fn).view(np.uint8) & 0xF
        words = c[..., 0::2] | (c[..., 1::2] << 4)
    return np.ascontiguousarray(words), np.ascontiguousarray(byte.astype(np.uint8).reshape(k // 512, 16, n))


def unpack_weight(words, scales, fmt):
    g, p, n, _ = words.shape
    if fmt == "e4m3":
        vals = np.ascontiguousarray(words).view(ml_dtypes.float8_e4m3fn).astype(np.float64)
    else:
        nib = np.empty((g, p, n, 4), np.uint8)
        nib[..., 0::2] = words & 0xF
        nib[..., 1::2] = words >> 4
        vals = E2M1[nib]
    vals = vals * np.repeat(np.exp2(scales.astype(np.float64) - 127.0), 8, axis=1)[..., None]
    return vals.transpose(0, 1, 3, 2).reshape(g * 512, n)
def pack4(w):
    words, scales = pack_weight(w, "e2m1")
    return words.reshape(words.shape[0], 128, -1), scales


def unpack4(words, scales):
    return unpack_weight(words.reshape(words.shape[0], 128, -1, 2), scales, "e2m1")


def planes(Y):
    n, m = Y.shape
    b = f64(bf(Y)).reshape(n // 32, 32, m)
    amax = np.abs(b).max(1)
    byte = np.clip(np.where(amax > 0, np.frexp(amax)[1] - 1 + 127 - 7, 1), 1, 254)
    codes = (b * np.exp2(127.0 - byte)[:, None, :]).reshape(n, m).astype(np.float32).astype(ml_dtypes.float8_e4m3fn).view(np.uint8)
    words = codes.reshape(n // 512, 128, 4, m).transpose(0, 1, 3, 2)
    return np.ascontiguousarray(words), np.ascontiguousarray(byte.astype(np.uint8).reshape(n // 512, 16, m))


M, C, H = 1536, 2048, 1024


def setup_inputs():
    s = mx_kscale(C)
    t = mx_kscale(H)
    spread = np.exp(0.8 * np.random.randn(H))
    err_t = np.random.randn(C, M) * s[:, None]
    e_words, e_scales = pack_weight(err_t, "e4m3")
    head_t = np.random.randn(C, H) / np.sqrt(C) / s[:, None] * t[None, :]
    head_words, head_scales = pack4(head_t)
    w_rec = np.random.randn(H, H) / np.sqrt(H) * spread[:, None] / t[None, :]
    return {
        "e_words": e_words,
        "e_scales": e_scales,
        "head_words": head_words,
        "head_scales": head_scales,
        "w_rec": bf(w_rec),
        "h_now": bf(np.tanh(0.6 * np.random.randn(M, H))),
        "h_prev": bf(np.tanh(0.6 * np.random.randn(M, H))),
        "grad_prev": bf(0.5 * np.random.randn(M, H) * spread[None, :]),
    }


def reference(e_words, e_scales, head_words, head_scales, w_rec, h_now, h_prev, grad_prev):
    err = unpack_weight(e_words, e_scales, "e4m3").T
    head_t = unpack4(head_words, head_scales)
    d_now = err @ head_t
    delta = d_now * (1.0 - f64(h_now) ** 2)
    d_rec = mxq(delta, 1, "e4m3") @ mxq(f64(w_rec), 1, "e4m3").T
    y = (d_rec + f64(grad_prev)) * (1.0 - f64(h_prev) ** 2)
    words, scales = planes(y.T)
    return y, words, scales

@@ -1,0 +1,446 @@
+from contextlib import ExitStack
+
+import concourse.mybir as mybir
+from concourse.masks import make_identity
+
+M, C, H = 1536, 2048, 1024
+FLOPS = 2 * M * C * H + 2 * M * H * H
+
+F32 = mybir.dt.float32
+BF16 = mybir.dt.bfloat16
+I32 = mybir.dt.int32
+U32 = mybir.dt.uint32
+U8 = mybir.dt.uint8
+FP8X4 = mybir.dt.float8_e4m3fn_x4
+FP4X4 = mybir.dt.float4_e2m1fn_x4
+ALU = mybir.AluOpType
+ACT = mybir.ActivationFunctionType
+
+P = 128
+BANK = 512
+TILES = M // P
+CG = C // 512
+HG = H // 512
+E_CHUNKS = [(0, 1), (1, 2), (2, 3), (3, 6), (6, 9), (9, 12)]
+ES_CHUNKS = [(0, 4), (4, 12)]
+CODE_CHUNKS = [(0, 4), (4, 8), (8, 11), (11, 12)]
+SCALE_CHUNKS = [(0, 11), (11, 12)]
+LAG = 2
+RING = 7
+SHARE = 0
+
+
+def chunk_of(chunks, s):
+    return [c for c in chunks if c[0] <= s < c[1]][0]
+
+
+def tile_rnn_step_backprop_h2_kernel(
+    tc, e_words, e_scales, head_words, head_scales, w_rec, h_now, h_prev, grad_prev, out_0, out_1, out_2
+):
+    nc = tc.nc
+    with ExitStack() as ctx:
+        keep = ctx.enter_context(tc.tile_pool(name="keep", bufs=1))
+        ring = ctx.enter_context(tc.tile_pool(name="ring", bufs=3))
+        psum = ctx.enter_context(tc.psum_pool(name="psum", bufs=8))
+        ctx.enter_context(tc.manual_schedule())
+
+        t = {}
+
+        def kept(name, shape, dtype):
+            t[name] = keep.tile(shape, dtype, name=name, align_bytes=64)
+            return t[name]
+
+        def rotating(tag, key, shape, dtype, bufs):
+            t[tag, key] = ring.tile(shape, dtype, name=tag, tag=tag, bufs=bufs, align_bytes=64)
+            return t[tag, key]
+
+        def bank(kind, key):
+            t[kind, key] = psum.tile([P, BANK], F32, name="bank", tag="bank")
+            return t[kind, key]
+
+        e_rows = e_words.rearrange("g p m t -> p g (m t)")
+        head_rows = head_words.rearrange("g p n -> p g n")
+        code_rows = out_1.rearrange("g p m t -> p g (m t)")
+
+        def load_e(c):
+            lo, hi = c
+            tile = kept("e%d" % lo, [P, CG, (hi - lo) * P], U32)
+            nc.sync.dma_start(out=tile[:].bitcast(I32), in_=e_rows[:, :, 4 * P * lo : 4 * P * hi].bitcast(I32))
+
+        def clear_plane(eng, name, width):
+            plane = kept(name, [P, CG, width], U8)
+            eng.memset(plane[:].bitcast(I32), 0)
+
+        def load_plane(queues, name, scales, lo, hi):
+            for q in range(4):
+                queues[q].dma_start(
+                    out=t[name][q:P:32, :, :].bitcast(I32),
+                    in_=scales[:, q:16:4, lo:hi].rearrange("g r n -> r g n").bitcast(I32),
+                )
+
+        def load_head(pair):
+            tile = kept("head%d" % pair, [P, 2, 2 * H], U8)
+            nc.sync.dma_start(out=tile[:].bitcast(I32), in_=head_rows[:, 2 * pair : 2 * pair + 2, :].bitcast(I32))
+
+        def load_w(pair):
+            tile = kept("w%d" % pair, [P, 2, H], BF16)
+            nc.sync.dma_start(out=tile[:], in_=w_rec[2 * P * pair : 2 * P * (pair + 1), :].rearrange("(r p) j -> p r j", p=P))
+
+        def load_rows(tag, src, s):
+            tile = rotating(tag, s, [P, H], BF16, RING)
+            nc.sync.dma_start(out=tile[:], in_=src[P * s : P * (s + 1), :])
+
+        def square(tag, s):
+            sq = rotating("sq_" + tag, s, [P, H], F32, 3 if tag == "now" else 4)
+            nc.scalar.activation(out=sq[:], in_=t[tag, s][:], func=ACT.Square)
+
+        def stage1(s, by_group=False):
+            lo = chunk_of(E_CHUNKS, s)[0]
+            slo = chunk_of(ES_CHUNKS, s)[0]
+            passes = [(g, h) for g in range(CG) for h in range(2)]
+            for g, h in passes if by_group else sorted(passes, key=lambda gh: gh[1]):
+                if g == 0:
+                    bank("d", (s, h))
+                nc.tensor.matmul_mx(
+                    out=t["d", (s, h)][:],
+                    lhsT=t["e%d" % lo][:, g, P * (s - lo) : P * (s - lo + 1)].bitcast(FP8X4),
+                    lhsT_scale=t["es%d" % slo][:, g, P * (s - slo) : P * (s - slo + 1)],
+                    rhs=t["head%d" % (g // 2)][:, g % 2, 2 * BANK * h : 2 * BANK * (h + 1)].bitcast(FP4X4),
+                    rhs_scale=t["hs"][:, g, BANK * h : BANK * (h + 1)],
+                    start=(g == 0),
+                    stop=(g == CG - 1),
+                )
+
+        def delta(s, h):
+            dbf = rotating("dbf", (s, h), [P, BANK], BF16, 6)
+            sq = t["sq_now", s][:, BANK * h : BANK * (h + 1)].rearrange("p (q u e) -> p u q e", u=2, e=16)
+            acc = t["d", (s, h)][:].rearrange("p (q u e) -> p u q e", u=2, e=16)
+            dst = dbf[:].rearrange("p (u q e) -> p u q e", u=2, e=16)
+            for u in range(2):
+                nc.vector.scalar_tensor_tensor(
+                    out=dst[:, u], in0=sq[:, u], scalar=1.0, in1=acc[:, u], op0=ALU.subtract, op1=ALU.mult
+                )
+
+        def turn(kind, key, sources):
+            dst = bank(kind, key)
+            for k, src in enumerate(sources):
+                nc.tensor.transpose(dst[:, P * k : P * (k + 1)], src, t["ident"][:])
+
+        def pairs(tile, k):
+            return tile[:].bitcast(F32)[:, P * k : P * (k + 1)]
+
+        def unload(kind, key, dst, n, copy=nc.scalar.copy):
+            src = t[kind, key][:, 0 : 2 * P * n].rearrange("p (n u m) -> p n m u", u=2, m=P)
+            copy(out=dst, in_=src)
+
+        def turn_delta(s):
+            turn("dT", s, [pairs(t["dbf", (s, n)], u) for n in range(HG) for u in range(2)])
+
+        def unload_delta(s):
+            dst = rotating("dTs", s, [P, 2 * P * HG], F32, 3)
+            unload("dT", s, dst[:].rearrange("p (n m u) -> p n m u", u=2, m=P), HG)
+
+        def quant_delta(s):
+            codes = rotating("dq", s, [P, HG * P], U32, LAG + 2)
+            scales = rotating("dsc", s, [P, HG * P], U8, LAG + 2)
+            nc.vector.quantize_mx(out=codes[:].bitcast(FP8X4), scales=scales[:], in_=t["dTs", s][:].bitcast(BF16))
+
+        def sort_w(r):
+            dst = rotating("ws", r, [P, H], BF16, 4)
+            nc.vector.tensor_copy(
+                out=dst[:].rearrange("p (n u q e) -> p n u q e", n=HG, u=2, e=16),
+                in_=t["w%d" % (r // 2)][:, r % 2, :].rearrange("p (n q u e) -> p n u q e", n=HG, u=2, e=16),
+            )
+
+        def turn_w(pair):
+            for n in range(HG):
+                turn("wT", (pair, n), [pairs(t["ws", 2 * pair + r], 2 * n + u) for r in range(2) for u in range(2)])
+
+        def unload_w(pair, n, copy=nc.scalar.copy):
+            h, half = divmod(pair, 2)
+            if half == 0:
+                kept("wT%d%d" % (h, n), [P, 2 * BANK], F32)
+            dst = t["wT%d%d" % (h, n)][:, BANK * half : BANK * (half + 1)].rearrange("p (r m u) -> p r m u", u=2, m=P)
+            unload("wT", (pair, n), dst, 2, copy)
+
+        def quant_w(h, n):
+            codes = kept("wq%d%d" % (h, n), [P, BANK], U32)
+            scales = kept("wsc%d%d" % (h, n), [P, BANK], U8)
+            nc.vector.quantize_mx(out=codes[:].bitcast(FP8X4), scales=scales[:], in_=t["wT%d%d" % (h, n)][:].bitcast(BF16))
+
+        def stage2(s, h):
+            acc = bank("r", (s, h))
+            for n in range(HG):
+                nc.tensor.matmul_mx(
+                    out=acc[:],
+                    lhsT=t["dq", s][:, P * n : P * (n + 1)].bitcast(FP8X4),
+                    lhsT_scale=t["dsc", s][:, P * n : P * (n + 1)],
+                    rhs=t["wq%d%d" % (h, n)][:].bitcast(FP8X4),
+                    rhs_scale=t["wsc%d%d" % (h, n)][:],
+                    start=(n == 0),
+                    stop=(n == HG - 1),
+                )
+
+        def add_grad(s, h):
+            total = rotating("total", (s, h), [P, BANK], F32, 4)
+            nc.vector.tensor_tensor(
+                out=total[:], in0=t["r", (s, h)][:], in1=t["grad", s][:, BANK * h : BANK * (h + 1)], op=ALU.subtract
+            )
+
+        def result(s, h, share=0):
+            if ("y", s) not in t:
+                rotating("y", s, [P, H], F32, 4)
+            cols = slice(BANK * h, BANK * (h + 1) - share)
+            nc.vector.scalar_tensor_tensor(
+                out=t["y", s][:, cols], in0=t["sq_prev", s][:, cols], scalar=1.0, in1=t["total", (s, h)][:, 0 : BANK - share],
+                op0=ALU.subtract, op1=ALU.mult,
+            )
+
+        def slope(s):
+            dst = rotating("slope", s, [P, SHARE], F32, 3)
+            nc.scalar.activation(out=dst[:], in_=t["sq_prev", s][:, H - SHARE : H], func=ACT.Copy, bias=-1.0)
+
+        def result_share(s):
+            rotating("y", s, [P, H], F32, 4)
+            nc.gpsimd.tensor_tensor(
+                out=t["y", s][:, H - SHARE : H], in0=t["slope", s][:], in1=t["total", (s, 1)][:, BANK - SHARE : BANK], op=ALU.mult
+            )
+
+        def round_y(s, on_scalar=False):
+            dst = rotating("ybf", s, [P, H], BF16, 3)[:].rearrange("p (u w e) -> p u w e", u=2, e=2)
+            src = t["y", s][:].rearrange("p (w u e) -> p u w e", u=2, e=2)
+            if on_scalar:
+                nc.scalar.copy(out=dst, in_=src)
+            else:
+                nc.gpsimd.tensor_scalar(out=dst, in0=src, scalar1=1.0, scalar2=0.0, op0=ALU.mult, op1=ALU.add)
+
+        def turn_y(s):
+            turn("yT", s, [pairs(t["ybf", s], HG * u + g) for g in range(HG) for u in range(2)])
+
+        def unload_y(s):
+            dst = rotating("yTs", s, [P, 2 * P * HG], F32, 3)
+            unload("yT", s, dst[:].rearrange("p (n m u) -> p n m u", u=2, m=P), HG)
+
+        def quant_y(s, g, src):
+            lo, hi = chunk_of(CODE_CHUNKS, s)
+            slo, shi = chunk_of(SCALE_CHUNKS, s)
+            if s == lo and g == 0:
+                kept("yq%d" % lo, [P, HG, P * (hi - lo)], U32)
+            if s == slo and g == 0:
+                kept("ysc%d" % slo, [P, HG, P * (shi - slo)], U8)
+            nc.vector.quantize_mx(
+                out=t["yq%d" % lo][:, g, P * (s - lo) : P * (s - lo + 1)].bitcast(FP8X4),
+                scales=t["ysc%d" % slo][:, g, P * (s - slo) : P * (s - slo + 1)],
+                in_=src.bitcast(BF16),
+            )
+
+        def quant_y_tile(s):
+            for g in range(HG):
+                quant_y(s, g, t["yTs", s][:, 2 * P * g : 2 * P * (g + 1)])
+
+        def round_half(s, g, eng):
+            dst = rotating("ybh", (s, g), [P, BANK], BF16, 2)
+            eng(
+                out=dst[:].rearrange("p (u w e) -> p u w e", u=2, e=2),
+                in_=t["y", s][:, BANK * g : BANK * (g + 1)].rearrange("p (w u e) -> p u w e", u=2, e=2),
+            )
+
+        def turn_half(s, g):
+            turn("yT", (s, g), [pairs(t["ybh", (s, g)], u) for u in range(2)])
+
+        def unload_half(s, g):
+            dst = rotating("yTh", (s, g), [P, 2 * P], F32, 2)
+            unload("yT", (s, g), dst[:].rearrange("p (n m u) -> p n m u", u=2, m=P), 1)
+
+        def store_y(s, lo=0, hi=H):
+            nc.sync.dma_start(out=out_0[P * s : P * (s + 1), lo:hi], in_=t["y", s][:, lo:hi])
+
+        def store_planes(s, queues):
+            lo, hi = chunk_of(CODE_CHUNKS, s)
+            if s == hi - 1:
+                nc.sync.dma_start(
+                    out=code_rows[:, :, 4 * P * lo : 4 * P * hi].bitcast(I32), in_=t["yq%d" % lo][:].bitcast(I32)
+                )
+            lo, hi = chunk_of(SCALE_CHUNKS, s)
+            if s == hi - 1:
+                for q in range(4):
+                    queues[q].dma_start(
+                        out=out_2[:, 4 * q : 4 * q + 4, P * lo : P * hi].rearrange("g r m -> r g m").bitcast(I32),
+                        in_=t["ysc%d" % lo][32 * q : 32 * q + 4, :, :].bitcast(I32),
+                    )
+
+        def valid(s):
+            return 0 <= s < TILES
+
+        clear_plane(nc.vector, "es0", P * 4)
+        clear_plane(nc.vector, "hs", H)
+        load_e(E_CHUNKS[0])
+        load_head(0)
+        load_plane([nc.scalar, nc.scalar, nc.gpsimd, nc.gpsimd], "es0", e_scales, 0, P * 4)
+        load_plane([nc.sync] * 4, "hs", head_scales, 0, H)
+        clear_plane(nc.vector, "es4", P * 8)
+        ident = kept("ident", [P, P], F32)
+        make_identity(nc, ident[:])
+        load_head(1)
+        load_rows("now", h_now, 0)
+        load_e(E_CHUNKS[1])
+        load_w(0)
+        load_rows("now", h_now, 1)
+        load_w(1)
+        load_e(E_CHUNKS[2])
+        load_w(2)
+        load_rows("now", h_now, 2)
+        load_w(3)
+        load_rows("prev", h_prev, 0)
+        load_rows("grad", grad_prev, 0)
+        load_e(E_CHUNKS[3])
+        load_rows("prev", h_prev, 1)
+        load_rows("grad", grad_prev, 1)
+        load_rows("now", h_now, 3)
+        load_plane([nc.sync] * 4, "es4", e_scales, P * 4, M)
+        for s in range(2, 5):
+            load_rows("now", h_now, s + 2)
+            load_rows("prev", h_prev, s)
+            load_rows("grad", grad_prev, s)
+
+        def deltas(s):
+            for h in range(2):
+                delta(s, h)
+
+        square("now", 0)
+        stage1(0)
+        deltas(0)
+        square("now", 1)
+        stage1(1)
+        for r in range(4):
+            sort_w(r)
+        turn_w(0)
+        turn_delta(0)
+        turn_w(1)
+        deltas(1)
+        for n in range(HG):
+            unload_w(0, n)
+        unload_delta(0)
+        unload_w(1, 0)
+        unload_w(1, 1, nc.vector.tensor_copy)
+        square("now", 2)
+        stage1(2)
+        for r in range(4, 6):
+            sort_w(r)
+        quant_delta(0)
+        for n in range(HG):
+            quant_w(0, n)
+        for r in range(6, 8):
+            sort_w(r)
+        stage2(0, 0)
+        turn_w(2)
+        turn_delta(1)
+        turn_w(3)
+        deltas(2)
+        square("prev", 0)
+        for n in range(HG):
+            unload_w(2, n)
+        unload_delta(1)
+        add_grad(0, 0)
+        unload_w(3, 0)
+        unload_w(3, 1, nc.vector.tensor_copy)
+        square("now", 3)
+        stage1(3)
+        result(0, 0)
+        quant_delta(1)
+        for n in range(HG):
+            quant_w(1, n)
+        stage2(0, 1)
+        stage2(1, 0)
+        stage2(1, 1)
+        turn_delta(2)
+        square("prev", 1)
+        if SHARE:
+            slope(1)
+        deltas(3)
+        add_grad(0, 1)
+        unload_delta(2)
+        square("now", 4)
+        quant_delta(2)
+        result(0, 1)
+        round_y(0)
+
+        last = TILES - 1
+        for s in range(4, TILES):
+            r, b = s - 3, s - 4
+            if valid(s + 3):
+                if s + 2 == chunk_of(E_CHUNKS, s + 2)[0]:
+                    load_e(chunk_of(E_CHUNKS, s + 2))
+                load_rows("now", h_now, s + 3)
+            if valid(s + 1):
+                load_rows("prev", h_prev, s + 1)
+                load_rows("grad", grad_prev, s + 1)
+            store_y(b)
+            if b > 0:
+                store_planes(b - 1, [nc.sync] * 4)
+            if valid(s + 1):
+                square("now", s + 1)
+            square("prev", r + 1)
+            if SHARE and s < last:
+                slope(r + 1)
+            if s == last:
+                square("prev", r + 2)
+            for h in range(2):
+                add_grad(r, h)
+            if SHARE:
+                result_share(r)
+            stage1(s)
+            deltas(s)
+            for h in range(2):
+                stage2(s - 2, h)
+            turn_delta(s - 1)
+            turn_y(b)
+            if s == last:
+                turn_delta(s)
+            unload_delta(s - 1)
+            unload_y(b)
+            result(r, 0)
+            quant_delta(s - 1)
+            quant_y_tile(b)
+            if s == last:
+                unload_delta(last)
+            result(r, 1, SHARE)
+            round_y(r)
+
+        quant_delta(last)
+        square("prev", last)
+        for r in range(last - 2, last):
+            store_y(r - 1)
+            store_planes(r - 2, [nc.sync] * 4)
+            for h in range(2):
+                add_grad(r, h)
+            for h in range(2):
+                stage2(r + 1, h)
+            turn_y(r - 1)
+            unload_y(r - 1)
+            result(r, 0)
+            result(r, 1)
+            round_y(r, on_scalar=True)
+            quant_y_tile(r - 1)
+        a = last - 1
+        store_y(a)
+        store_planes(a - 1, [nc.sync] * 4)
+        for h in range(2):
+            add_grad(last, h)
+        turn_y(a)
+        unload_y(a)
+        result(last, 0)
+        store_y(last, 0, BANK)
+        round_half(last, 0, nc.scalar.copy)
+        result(last, 1)
+        store_y(last, BANK, H)
+        turn_half(last, 0)
+        quant_y_tile(a)
+        round_half(last, 1, nc.vector.tensor_copy)
+        store_planes(a, [nc.sync] * 4)
+        unload_half(last, 0)
+        turn_half(last, 1)
+        unload_half(last, 1)
+        for g in range(HG):
+            quant_y(last, g, t["yTh", (last, g)][:])
+        store_planes(last, [nc.scalar, nc.sync, nc.scalar, nc.sync])

@@ -23,11 +23,14 @@ CG = C // 512
 HG = H // 512
 E_CHUNKS = [(0, 1), (1, 2), (2, 3), (3, 6), (6, 9), (9, 12)]
 ES_CHUNKS = [(0, 4), (4, 12)]
-CODE_CHUNKS = [(0, 4), (4, 8), (8, 11), (11, 12)]
-SCALE_CHUNKS = [(0, 11), (11, 12)]
+QUANT_CHUNKS = [(0, 2), (2, 4), (4, 6), (6, 8), (8, 10), (10, 11), (11, 12)]
+CODE_CHUNKS = [(0, 4), (4, 8), (8, 10), (10, 11), (11, 12)]
+SCALE_CHUNKS = [(0, 10), (10, 12)]
 LAG = 2
 RING = 7
 SHARE = 0
+W_ON_V = 0
+ON_GPSIMD = True
 
 
 def chunk_of(chunks, s):
@@ -91,7 +94,7 @@ def tile_rnn_step_backprop_h2_kernel(
             nc.sync.dma_start(out=tile[:], in_=src[P * s : P * (s + 1), :])
 
         def square(tag, s):
-            sq = rotating("sq_" + tag, s, [P, H], F32, 3 if tag == "now" else 4)
+            sq = rotating("sq_" + tag, s, [P, H], F32, 3)
             nc.scalar.activation(out=sq[:], in_=t[tag, s][:], func=ACT.Square)
 
         def stage1(s, by_group=False):
@@ -145,16 +148,16 @@ def tile_rnn_step_backprop_h2_kernel(
             scales = rotating("dsc", s, [P, HG * P], U8, LAG + 2)
             nc.vector.quantize_mx(out=codes[:].bitcast(FP8X4), scales=scales[:], in_=t["dTs", s][:].bitcast(BF16))
 
-        def sort_w(r):
-            dst = rotating("ws", r, [P, H], BF16, 4)
+        def sort_w(pair):
+            dst = rotating("ws", pair, [P, 2 * H], BF16, 2)
             nc.vector.tensor_copy(
-                out=dst[:].rearrange("p (n u q e) -> p n u q e", n=HG, u=2, e=16),
-                in_=t["w%d" % (r // 2)][:, r % 2, :].rearrange("p (n q u e) -> p n u q e", n=HG, u=2, e=16),
+                out=dst[:].rearrange("p (n u q e) -> p n u q e", n=2 * HG, u=2, e=16),
+                in_=t["w%d" % pair][:].rearrange("p r (n q u e) -> p (r n) u q e", n=HG, u=2, e=16),
             )
 
         def turn_w(pair):
             for n in range(HG):
-                turn("wT", (pair, n), [pairs(t["ws", 2 * pair + r], 2 * n + u) for r in range(2) for u in range(2)])
+                turn("wT", (pair, n), [pairs(t["ws", pair], 2 * HG * r + 2 * n + u) for r in range(2) for u in range(2)])
 
         def unload_w(pair, n, copy=nc.scalar.copy):
             h, half = divmod(pair, 2)
@@ -182,17 +185,16 @@ def tile_rnn_step_backprop_h2_kernel(
                 )
 
         def add_grad(s, h):
-            total = rotating("total", (s, h), [P, BANK], F32, 4)
-            nc.vector.tensor_tensor(
-                out=total[:], in0=t["r", (s, h)][:], in1=t["grad", s][:, BANK * h : BANK * (h + 1)], op=ALU.subtract
-            )
+            if ("total", s) not in t:
+                rotating("total", s, [P, H], F32, 2)
+            cols = slice(BANK * h, BANK * (h + 1))
+            nc.vector.tensor_tensor(out=t["total", s][:, cols], in0=t["r", (s, h)][:], in1=t["grad", s][:, cols], op=ALU.subtract)
 
-        def result(s, h, share=0):
+        def result(s, lo=0, hi=H):
             if ("y", s) not in t:
                 rotating("y", s, [P, H], F32, 4)
-            cols = slice(BANK * h, BANK * (h + 1) - share)
             nc.vector.scalar_tensor_tensor(
-                out=t["y", s][:, cols], in0=t["sq_prev", s][:, cols], scalar=1.0, in1=t["total", (s, h)][:, 0 : BANK - share],
+                out=t["y", s][:, lo:hi], in0=t["sq_prev", s][:, lo:hi], scalar=1.0, in1=t["total", s][:, lo:hi],
                 op0=ALU.subtract, op1=ALU.mult,
             )
 
@@ -203,54 +205,49 @@ def tile_rnn_step_backprop_h2_kernel(
         def result_share(s):
             rotating("y", s, [P, H], F32, 4)
             nc.gpsimd.tensor_tensor(
-                out=t["y", s][:, H - SHARE : H], in0=t["slope", s][:], in1=t["total", (s, 1)][:, BANK - SHARE : BANK], op=ALU.mult
+                out=t["y", s][:, H - SHARE : H], in0=t["slope", s][:], in1=t["total", s][:, H - SHARE : H], op=ALU.mult
             )
 
-        def round_y(s, on_scalar=False):
-            dst = rotating("ybf", s, [P, H], BF16, 3)[:].rearrange("p (u w e) -> p u w e", u=2, e=2)
-            src = t["y", s][:].rearrange("p (w u e) -> p u w e", u=2, e=2)
-            if on_scalar:
-                nc.scalar.copy(out=dst, in_=src)
-            else:
-                nc.gpsimd.tensor_scalar(out=dst, in0=src, scalar1=1.0, scalar2=0.0, op0=ALU.mult, op1=ALU.add)
+        def gpsimd_copy(out, in_):
+            nc.gpsimd.tensor_scalar(out=out, in0=in_, scalar1=1.0, scalar2=0.0, op0=ALU.mult, op1=ALU.add)
 
-        def turn_y(s):
-            turn("yT", s, [pairs(t["ybf", s], HG * u + g) for g in range(HG) for u in range(2)])
-
-        def unload_y(s):
-            dst = rotating("yTs", s, [P, 2 * P * HG], F32, 3)
-            unload("yT", s, dst[:].rearrange("p (n m u) -> p n m u", u=2, m=P), HG)
-
-        def quant_y(s, g, src):
-            lo, hi = chunk_of(CODE_CHUNKS, s)
-            slo, shi = chunk_of(SCALE_CHUNKS, s)
-            if s == lo and g == 0:
-                kept("yq%d" % lo, [P, HG, P * (hi - lo)], U32)
-            if s == slo and g == 0:
-                kept("ysc%d" % slo, [P, HG, P * (shi - slo)], U8)
-            nc.vector.quantize_mx(
-                out=t["yq%d" % lo][:, g, P * (s - lo) : P * (s - lo + 1)].bitcast(FP8X4),
-                scales=t["ysc%d" % slo][:, g, P * (s - slo) : P * (s - slo + 1)],
-                in_=src.bitcast(BF16),
-            )
-
-        def quant_y_tile(s):
-            for g in range(HG):
-                quant_y(s, g, t["yTs", s][:, 2 * P * g : 2 * P * (g + 1)])
-
-        def round_half(s, g, eng):
-            dst = rotating("ybh", (s, g), [P, BANK], BF16, 2)
-            eng(
+        def round_y(s, g, copy):
+            dst = rotating("ybf", (s, g), [P, BANK], BF16, 6)
+            copy(
                 out=dst[:].rearrange("p (u w e) -> p u w e", u=2, e=2),
                 in_=t["y", s][:, BANK * g : BANK * (g + 1)].rearrange("p (w u e) -> p u w e", u=2, e=2),
             )
 
-        def turn_half(s, g):
-            turn("yT", (s, g), [pairs(t["ybh", (s, g)], u) for u in range(2)])
+        def rounding(s):
+            round_y(s, 1, gpsimd_copy if ON_GPSIMD else nc.scalar.copy)
+            round_y(s, 0, nc.scalar.copy)
 
-        def unload_half(s, g):
-            dst = rotating("yTh", (s, g), [P, 2 * P], F32, 2)
-            unload("yT", (s, g), dst[:].rearrange("p (n m u) -> p n m u", u=2, m=P), 1)
+        def turn_y(s, groups=(0, 1)):
+            turn("yT", (s, groups), [pairs(t["ybf", (s, g)], u) for g in groups for u in range(2)])
+
+        def unload_y(s, groups=(0, 1), copy=nc.scalar.copy):
+            lo, hi = chunk_of(QUANT_CHUNKS, s)
+            if ("yTs", lo) not in t:
+                rotating("yTs", lo, [P, HG, 4 * P], F32, 3)
+            dst = t["yTs", lo][:, groups[0] : groups[-1] + 1, 2 * P * (s - lo) : 2 * P * (s - lo + 1)]
+            unload("yT", (s, groups), dst.rearrange("p n (m u) -> p n m u", u=2), len(groups), copy)
+
+        def quant_y(s, groups=(0, 1)):
+            first, end = chunk_of(QUANT_CHUNKS, s)
+            if s != end - 1:
+                return
+            lo, hi = chunk_of(CODE_CHUNKS, s)
+            slo, shi = chunk_of(SCALE_CHUNKS, s)
+            if "yq%d" % lo not in t:
+                kept("yq%d" % lo, [P, HG, P * (hi - lo)], U32)
+            if "ysc%d" % slo not in t:
+                kept("ysc%d" % slo, [P, HG, P * (shi - slo)], U8)
+            for g in groups:
+                nc.vector.quantize_mx(
+                    out=t["yq%d" % lo][:, g, P * (first - lo) : P * (end - lo)].bitcast(FP8X4),
+                    scales=t["ysc%d" % slo][:, g, P * (first - slo) : P * (end - slo)],
+                    in_=t["yTs", first][:, g, 0 : 2 * P * (end - first)].bitcast(BF16),
+                )
 
         def store_y(s, lo=0, hi=H):
             nc.sync.dma_start(out=out_0[P * s : P * (s + 1), lo:hi], in_=t["y", s][:, lo:hi])
@@ -312,8 +309,8 @@ def tile_rnn_step_backprop_h2_kernel(
         deltas(0)
         square("now", 1)
         stage1(1)
-        for r in range(4):
-            sort_w(r)
+        sort_w(0)
+        sort_w(1)
         turn_w(0)
         turn_delta(0)
         turn_w(1)
@@ -322,16 +319,14 @@ def tile_rnn_step_backprop_h2_kernel(
             unload_w(0, n)
         unload_delta(0)
         unload_w(1, 0)
-        unload_w(1, 1, nc.vector.tensor_copy)
+        unload_w(1, 1, nc.vector.tensor_copy if W_ON_V & 1 else nc.scalar.copy)
         square("now", 2)
         stage1(2)
-        for r in range(4, 6):
-            sort_w(r)
+        sort_w(2)
         quant_delta(0)
         for n in range(HG):
             quant_w(0, n)
-        for r in range(6, 8):
-            sort_w(r)
+        sort_w(3)
         stage2(0, 0)
         turn_w(2)
         turn_delta(1)
@@ -343,30 +338,31 @@ def tile_rnn_step_backprop_h2_kernel(
         unload_delta(1)
         add_grad(0, 0)
         unload_w(3, 0)
-        unload_w(3, 1, nc.vector.tensor_copy)
+        unload_w(3, 1, nc.vector.tensor_copy if W_ON_V & 2 else nc.scalar.copy)
         square("now", 3)
-        stage1(3)
-        result(0, 0)
+        result(0, 0, BANK)
         quant_delta(1)
         for n in range(HG):
             quant_w(1, n)
-        stage2(0, 1)
-        stage2(1, 0)
-        stage2(1, 1)
-        turn_delta(2)
         square("prev", 1)
         if SHARE:
             slope(1)
+        stage1(3)
         deltas(3)
+        stage2(0, 1)
         add_grad(0, 1)
+        turn_delta(2)
         unload_delta(2)
         square("now", 4)
-        quant_delta(2)
-        result(0, 1)
-        round_y(0)
+        result(0, BANK, H)
+        square("now", 5)
+        rounding(0)
+        square("prev", 2)
+        if SHARE:
+            slope(2)
 
         last = TILES - 1
-        for s in range(4, TILES):
+        for s in range(4, TILES + 2):
             r, b = s - 3, s - 4
             if valid(s + 3):
                 if s + 2 == chunk_of(E_CHUNKS, s + 2)[0]:
@@ -376,71 +372,57 @@ def tile_rnn_step_backprop_h2_kernel(
                 load_rows("prev", h_prev, s + 1)
                 load_rows("grad", grad_prev, s + 1)
             store_y(b)
-            if b > 0:
-                store_planes(b - 1, [nc.sync] * 4)
-            if valid(s + 1):
-                square("now", s + 1)
-            square("prev", r + 1)
-            if SHARE and s < last:
-                slope(r + 1)
-            if s == last:
-                square("prev", r + 2)
+            if b > 1:
+                store_planes(b - 2, [nc.sync] * 4)
+            share = SHARE if valid(s) else 0
+            if valid(s):
+                stage1(s)
+                deltas(s)
+            for h in range(2):
+                stage2(r, h)
             for h in range(2):
                 add_grad(r, h)
-            if SHARE:
+            if share:
                 result_share(r)
-            stage1(s)
-            deltas(s)
-            for h in range(2):
-                stage2(s - 2, h)
-            turn_delta(s - 1)
+            quant_delta(s - 2)
+            if b > 0:
+                quant_y(b - 1)
+            result(r, 0, H - share)
+            if valid(s - 1):
+                turn_delta(s - 1)
             turn_y(b)
-            if s == last:
-                turn_delta(s)
-            unload_delta(s - 1)
+            if valid(s - 1):
+                unload_delta(s - 1)
             unload_y(b)
-            result(r, 0)
-            quant_delta(s - 1)
-            quant_y_tile(b)
-            if s == last:
-                unload_delta(last)
-            result(r, 1, SHARE)
-            round_y(r)
+            if valid(s + 2):
+                square("now", s + 2)
+            rounding(r)
+            if valid(s - 1):
+                square("prev", s - 1)
+            if SHARE and valid(s + 2):
+                slope(s - 1)
 
-        quant_delta(last)
-        square("prev", last)
-        for r in range(last - 2, last):
-            store_y(r - 1)
-            store_planes(r - 2, [nc.sync] * 4)
-            for h in range(2):
-                add_grad(r, h)
-            for h in range(2):
-                stage2(r + 1, h)
-            turn_y(r - 1)
-            unload_y(r - 1)
-            result(r, 0)
-            result(r, 1)
-            round_y(r, on_scalar=True)
-            quant_y_tile(r - 1)
-        a = last - 1
-        store_y(a)
-        store_planes(a - 1, [nc.sync] * 4)
+        store_y(last - 1)
+        for h in range(2):
+            stage2(last, h)
         for h in range(2):
             add_grad(last, h)
-        turn_y(a)
-        unload_y(a)
-        result(last, 0)
+        quant_y(last - 2)
+        store_planes(last - 2, [nc.sync] * 4)
+        turn_y(last - 1)
+        unload_y(last - 1)
+        result(last, 0, BANK)
         store_y(last, 0, BANK)
-        round_half(last, 0, nc.scalar.copy)
-        result(last, 1)
+        round_y(last, 0, nc.scalar.copy)
+        result(last, BANK, H)
         store_y(last, BANK, H)
-        turn_half(last, 0)
-        quant_y_tile(a)
-        round_half(last, 1, nc.vector.tensor_copy)
-        store_planes(a, [nc.sync] * 4)
-        unload_half(last, 0)
-        turn_half(last, 1)
-        unload_half(last, 1)
-        for g in range(HG):
-            quant_y(last, g, t["yTh", (last, g)][:])
+        turn_y(last, (0,))
+        quant_y(last - 1, (0,))
+        round_y(last, 1, nc.vector.tensor_copy)
+        quant_y(last - 1, (1,))
+        store_planes(last - 1, [nc.sync] * 4)
+        unload_y(last, (0,))
+        turn_y(last, (1,))
+        unload_y(last, (1,))
+        quant_y(last)
         store_planes(last, [nc.scalar, nc.sync, nc.scalar, nc.sync])

@@ -21,16 +21,16 @@ BANK = 512
 TILES = M // P
 CG = C // 512
 HG = H // 512
-E_CHUNKS = [(0, 1), (1, 2), (2, 3), (3, 6), (6, 9), (9, 12)]
-ES_CHUNKS = [(0, 4), (4, 12)]
-QUANT_CHUNKS = [(0, 2), (2, 4), (4, 6), (6, 8), (8, 10), (10, 11), (11, 12)]
-CODE_CHUNKS = [(0, 4), (4, 8), (8, 10), (10, 11), (11, 12)]
-SCALE_CHUNKS = [(0, 10), (10, 12)]
+E_CHUNKS = [(0, 1), (1, 3), (3, 6), (6, 9), (9, 12)]
+ES_CHUNKS = [(0, 3), (3, 12)]
+QUANT_CHUNKS = [(0, 2), (2, 4), (4, 6), (6, 8), (8, 9), (9, 10), (10, 11), (11, 12)]
+CODE_CHUNKS = [(0, 4), (4, 9), (9, 11), (11, 12)]
+SCALE_CHUNKS = [(0, 9), (9, 12)]
 LAG = 2
-RING = 7
-SHARE = 0
+RING = 6
 W_ON_V = 0
-ON_GPSIMD = True
+CATCH = 9
+SHARE = 0
 
 
 def chunk_of(chunks, s):
@@ -81,9 +81,9 @@ def tile_rnn_step_backprop_h2_kernel(
                     in_=scales[:, q:16:4, lo:hi].rearrange("g r n -> r g n").bitcast(I32),
                 )
 
-        def load_head(pair):
-            tile = kept("head%d" % pair, [P, 2, 2 * H], U8)
-            nc.sync.dma_start(out=tile[:].bitcast(I32), in_=head_rows[:, 2 * pair : 2 * pair + 2, :].bitcast(I32))
+        def load_head(h):
+            tile = kept("head%d" % h, [P, CG, 2 * BANK], U8)
+            nc.sync.dma_start(out=tile[:].bitcast(I32), in_=head_rows[:, :, 2 * BANK * h : 2 * BANK * (h + 1)].bitcast(I32))
 
         def load_w(pair):
             tile = kept("w%d" % pair, [P, 2, H], BF16)
@@ -97,19 +97,18 @@ def tile_rnn_step_backprop_h2_kernel(
             sq = rotating("sq_" + tag, s, [P, H], F32, 3)
             nc.scalar.activation(out=sq[:], in_=t[tag, s][:], func=ACT.Square)
 
-        def stage1(s, by_group=False):
+        def stage1(s, halves=(0, 1)):
             lo = chunk_of(E_CHUNKS, s)[0]
             slo = chunk_of(ES_CHUNKS, s)[0]
-            passes = [(g, h) for g in range(CG) for h in range(2)]
-            for g, h in passes if by_group else sorted(passes, key=lambda gh: gh[1]):
+            for h, g in [(h, g) for h in halves for g in range(CG)]:
                 if g == 0:
                     bank("d", (s, h))
                 nc.tensor.matmul_mx(
                     out=t["d", (s, h)][:],
                     lhsT=t["e%d" % lo][:, g, P * (s - lo) : P * (s - lo + 1)].bitcast(FP8X4),
                     lhsT_scale=t["es%d" % slo][:, g, P * (s - slo) : P * (s - slo + 1)],
-                    rhs=t["head%d" % (g // 2)][:, g % 2, 2 * BANK * h : 2 * BANK * (h + 1)].bitcast(FP4X4),
-                    rhs_scale=t["hs"][:, g, BANK * h : BANK * (h + 1)],
+                    rhs=t["head%d" % h][:, g, :].bitcast(FP4X4),
+                    rhs_scale=t["hs%d" % h][:, g, :],
                     start=(g == 0),
                     stop=(g == CG - 1),
                 )
@@ -136,17 +135,21 @@ def tile_rnn_step_backprop_h2_kernel(
             src = t[kind, key][:, 0 : 2 * P * n].rearrange("p (n u m) -> p n m u", u=2, m=P)
             copy(out=dst, in_=src)
 
-        def turn_delta(s):
-            turn("dT", s, [pairs(t["dbf", (s, n)], u) for n in range(HG) for u in range(2)])
+        def turn_delta(s, passes=(0, 1)):
+            turn("dT", (s, passes), [pairs(t["dbf", (s, n)], u) for n in passes for u in range(2)])
 
-        def unload_delta(s):
-            dst = rotating("dTs", s, [P, 2 * P * HG], F32, 3)
-            unload("dT", s, dst[:].rearrange("p (n m u) -> p n m u", u=2, m=P), HG)
+        def unload_delta(s, passes=(0, 1)):
+            dst = rotating("dTs", (s, passes), [P, 2 * P * len(passes)], F32, 3)
+            unload("dT", (s, passes), dst[:].rearrange("p (n m u) -> p n m u", u=2, m=P), len(passes))
 
-        def quant_delta(s):
-            codes = rotating("dq", s, [P, HG * P], U32, LAG + 2)
-            scales = rotating("dsc", s, [P, HG * P], U8, LAG + 2)
-            nc.vector.quantize_mx(out=codes[:].bitcast(FP8X4), scales=scales[:], in_=t["dTs", s][:].bitcast(BF16))
+        def quant_delta(s, passes=(0, 1)):
+            if ("dq", s) not in t:
+                rotating("dq", s, [P, HG * P], U32, 4)
+                rotating("dsc", s, [P, HG * P], U8, 4)
+            cols = slice(P * passes[0], P * (passes[-1] + 1))
+            nc.vector.quantize_mx(
+                out=t["dq", s][:, cols].bitcast(FP8X4), scales=t["dsc", s][:, cols], in_=t["dTs", (s, passes)][:].bitcast(BF16)
+            )
 
         def sort_w(pair):
             dst = rotating("ws", pair, [P, 2 * H], BF16, 2)
@@ -186,7 +189,7 @@ def tile_rnn_step_backprop_h2_kernel(
 
         def add_grad(s, h):
             if ("total", s) not in t:
-                rotating("total", s, [P, H], F32, 2)
+                rotating("total", s, [P, H], F32, 3)
             cols = slice(BANK * h, BANK * (h + 1))
             nc.vector.tensor_tensor(out=t["total", s][:, cols], in0=t["r", (s, h)][:], in1=t["grad", s][:, cols], op=ALU.subtract)
 
@@ -203,7 +206,6 @@ def tile_rnn_step_backprop_h2_kernel(
             nc.scalar.activation(out=dst[:], in_=t["sq_prev", s][:, H - SHARE : H], func=ACT.Copy, bias=-1.0)
 
         def result_share(s):
-            rotating("y", s, [P, H], F32, 4)
             nc.gpsimd.tensor_tensor(
                 out=t["y", s][:, H - SHARE : H], in0=t["slope", s][:], in1=t["total", s][:, H - SHARE : H], op=ALU.mult
             )
@@ -217,10 +219,6 @@ def tile_rnn_step_backprop_h2_kernel(
                 out=dst[:].rearrange("p (u w e) -> p u w e", u=2, e=2),
                 in_=t["y", s][:, BANK * g : BANK * (g + 1)].rearrange("p (w u e) -> p u w e", u=2, e=2),
             )
-
-        def rounding(s):
-            round_y(s, 1, gpsimd_copy if ON_GPSIMD else nc.scalar.copy)
-            round_y(s, 0, nc.scalar.copy)
 
         def turn_y(s, groups=(0, 1)):
             turn("yT", (s, groups), [pairs(t["ybf", (s, g)], u) for g in groups for u in range(2)])
@@ -269,157 +267,230 @@ def tile_rnn_step_backprop_h2_kernel(
         def valid(s):
             return 0 <= s < TILES
 
-        clear_plane(nc.vector, "es0", P * 4)
-        clear_plane(nc.vector, "hs", H)
-        load_e(E_CHUNKS[0])
-        load_head(0)
-        load_plane([nc.scalar, nc.scalar, nc.gpsimd, nc.gpsimd], "es0", e_scales, 0, P * 4)
-        load_plane([nc.sync] * 4, "hs", head_scales, 0, H)
-        clear_plane(nc.vector, "es4", P * 8)
-        ident = kept("ident", [P, P], F32)
-        make_identity(nc, ident[:])
-        load_head(1)
-        load_rows("now", h_now, 0)
-        load_e(E_CHUNKS[1])
-        load_w(0)
-        load_rows("now", h_now, 1)
-        load_w(1)
-        load_e(E_CHUNKS[2])
-        load_w(2)
-        load_rows("now", h_now, 2)
-        load_w(3)
-        load_rows("prev", h_prev, 0)
-        load_rows("grad", grad_prev, 0)
-        load_e(E_CHUNKS[3])
-        load_rows("prev", h_prev, 1)
-        load_rows("grad", grad_prev, 1)
-        load_rows("now", h_now, 3)
-        load_plane([nc.sync] * 4, "es4", e_scales, P * 4, M)
-        for s in range(2, 5):
-            load_rows("now", h_now, s + 2)
-            load_rows("prev", h_prev, s)
-            load_rows("grad", grad_prev, s)
+        def finish(r):
+            round_y(r, 1, gpsimd_copy)
+            round_y(r, 0, nc.scalar.copy)
 
         def deltas(s):
             for h in range(2):
                 delta(s, h)
 
+        clear_plane(nc.vector, "es0", P * 3)
+        clear_plane(nc.vector, "hs0", BANK)
+        clear_plane(nc.vector, "hs1", BANK)
+        load_e(E_CHUNKS[0])
+        load_plane([nc.gpsimd, nc.gpsimd, nc.scalar, nc.scalar], "es0", e_scales, 0, P * 3)
+        load_plane([nc.scalar] * 4, "hs0", head_scales, 0, BANK)
+        load_head(0)
+        load_plane([nc.gpsimd] * 4, "hs1", head_scales, BANK, H)
+        ident = kept("ident", [P, P], F32)
+        make_identity(nc, ident[:])
+        clear_plane(nc.gpsimd, "es3", P * 9)
+        load_head(1)
+        load_rows("now", h_now, 0)
+        load_e(E_CHUNKS[1])
+        load_w(0)
+        load_rows("now", h_now, 1)
+        for pair in range(1, 4):
+            load_w(pair)
+        load_rows("now", h_now, 2)
+        load_rows("prev", h_prev, 0)
+        load_rows("grad", grad_prev, 0)
+        load_plane([nc.sync] * 4, "es3", e_scales, P * 3, M)
+        load_e(E_CHUNKS[2])
+        load_rows("prev", h_prev, 1)
+        load_rows("grad", grad_prev, 1)
+        load_rows("now", h_now, 3)
+        for s in range(2, 5):
+            if s < 4:
+                load_rows("now", h_now, s + 2)
+            load_rows("prev", h_prev, s)
+            load_rows("grad", grad_prev, s)
+
         square("now", 0)
         stage1(0)
         deltas(0)
-        square("now", 1)
-        stage1(1)
         sort_w(0)
-        sort_w(1)
+        square("now", 1)
+        stage1(1, (0,))
         turn_w(0)
         turn_delta(0)
-        turn_w(1)
-        deltas(1)
         for n in range(HG):
             unload_w(0, n)
+        sort_w(1)
+        delta(1, 0)
+        stage1(1, (1,))
+        turn_w(1)
         unload_delta(0)
-        unload_w(1, 0)
-        unload_w(1, 1, nc.vector.tensor_copy if W_ON_V & 1 else nc.scalar.copy)
-        square("now", 2)
-        stage1(2)
+        for n in range(HG):
+            unload_w(1, n)
+        delta(1, 1)
         sort_w(2)
+        square("now", 2)
+        stage1(2, (0,))
+        turn_w(2)
+        turn_delta(1)
+        sort_w(3)
         quant_delta(0)
         for n in range(HG):
             quant_w(0, n)
-        sort_w(3)
-        stage2(0, 0)
-        turn_w(2)
-        turn_delta(1)
+        stage1(2, (1,))
         turn_w(3)
-        deltas(2)
-        square("prev", 0)
         for n in range(HG):
             unload_w(2, n)
-        unload_delta(1)
-        add_grad(0, 0)
+        deltas(2)
         unload_w(3, 0)
         unload_w(3, 1, nc.vector.tensor_copy if W_ON_V & 2 else nc.scalar.copy)
+        unload_delta(1)
+        stage2(0, 0)
+        square("prev", 0)
+        add_grad(0, 0)
+        for n in range(HG):
+            quant_w(1, n)
         square("now", 3)
         result(0, 0, BANK)
         quant_delta(1)
-        for n in range(HG):
-            quant_w(1, n)
-        square("prev", 1)
-        if SHARE:
-            slope(1)
         stage1(3)
-        deltas(3)
         stage2(0, 1)
-        add_grad(0, 1)
-        turn_delta(2)
-        unload_delta(2)
+        square("prev", 1)
         square("now", 4)
+        add_grad(0, 1)
+        deltas(3)
         result(0, BANK, H)
-        square("now", 5)
-        rounding(0)
-        square("prev", 2)
-        if SHARE:
-            slope(2)
+        finish(0)
+
+        def loads(s):
+            if valid(s + 3):
+                if s + 3 == chunk_of(E_CHUNKS, s + 3)[0]:
+                    load_e(chunk_of(E_CHUNKS, s + 3))
+                load_rows("now", h_now, s + 3)
+            if valid(s + 2):
+                load_rows("prev", h_prev, s + 2)
+                load_rows("grad", grad_prev, s + 2)
+
+        def both(f, r):
+            for h in range(2):
+                f(r, h)
 
         last = TILES - 1
-        for s in range(4, TILES + 2):
-            r, b = s - 3, s - 4
-            if valid(s + 3):
-                if s + 2 == chunk_of(E_CHUNKS, s + 2)[0]:
-                    load_e(chunk_of(E_CHUNKS, s + 2))
-                load_rows("now", h_now, s + 3)
-            if valid(s + 1):
-                load_rows("prev", h_prev, s + 1)
-                load_rows("grad", grad_prev, s + 1)
-            store_y(b)
-            if b > 1:
+        for s in range(3, CATCH):
+            r, b = s - 2, s - 4
+            loads(s)
+            store_y(r - 1)
+            if valid(b - 2):
                 store_planes(b - 2, [nc.sync] * 4)
-            share = SHARE if valid(s) else 0
-            if valid(s):
+            if s > 3:
                 stage1(s)
                 deltas(s)
-            for h in range(2):
-                stage2(r, h)
-            for h in range(2):
-                add_grad(r, h)
-            if share:
-                result_share(r)
-            quant_delta(s - 2)
-            if b > 0:
+            both(stage2, r)
+            both(add_grad, r)
+            turn_delta(s - 1)
+            if valid(b):
+                turn_y(b)
+            if s == CATCH - 1:
+                turn_delta(s)
+            unload_delta(s - 1)
+            if valid(b):
+                unload_y(b)
+            if s == CATCH - 1:
+                unload_delta(s)
+            square("now", s + 2)
+            square("prev", r + 1)
+            if valid(b - 1):
                 quant_y(b - 1)
-            result(r, 0, H - share)
-            if valid(s - 1):
-                turn_delta(s - 1)
-            turn_y(b)
-            if valid(s - 1):
-                unload_delta(s - 1)
-            unload_y(b)
+            quant_delta(s - 1)
+            result(r)
+            finish(r)
+
+        s = CATCH
+        quant_delta(s - 1)
+        loads(s)
+        store_y(s - 3)
+        if valid(s - 6):
+            store_planes(s - 6, [nc.sync] * 4)
+        square("prev", s - 1)
+        stage1(s)
+        deltas(s)
+        both(stage2, s - 2)
+        both(stage2, s - 1)
+        both(add_grad, s - 2)
+        turn_y(s - 4)
+        turn_delta(s)
+        turn_y(s - 3)
+        unload_y(s - 4)
+        unload_delta(s)
+        unload_y(s - 3)
+        quant_y(s - 5)
+        result(s - 2)
+        both(add_grad, s - 1)
+        finish(s - 2)
+        square("now", s + 2)
+        square("prev", s)
+        quant_delta(s)
+        quant_y(s - 4)
+        store_y(s - 2)
+        for b in (s - 5, s - 4):
+            store_planes(b, [nc.sync] * 4)
+
+        for s in range(CATCH + 1, TILES):
+            r = s - 1
+            bs = [s - 3, s - 2] if s == CATCH + 1 else [s - 2]
+            loads(s)
+            stage1(s)
+            delta(s, 0)
+            if s == CATCH + 1:
+                result(s - 2)
+                finish(s - 2)
+            quant_y(bs[0] - 1)
+            delta(s, 1)
+            store_y(r - 1)
+            store_planes(bs[0] - 1, [nc.sync] * 4)
+            both(stage2, r)
+            both(add_grad, r)
+            if s == last:
+                for n in range(HG):
+                    turn_delta(s, (n,))
+                    unload_delta(s, (n,))
+                    quant_delta(s, (n,))
+            for b in bs:
+                turn_y(b)
+            if s < last:
+                turn_delta(s)
+            unload_y(bs[0])
+            if s < last:
+                unload_delta(s)
+            for b in bs[1:]:
+                unload_y(b)
+                quant_y(b - 1)
+                store_planes(b - 1, [nc.sync] * 4)
+            result(r, 0, BANK)
+            result(r, BANK, H)
+            if s < last:
+                quant_delta(s)
+            if s == last:
+                square("prev", s)
+            finish(r)
             if valid(s + 2):
                 square("now", s + 2)
-            rounding(r)
-            if valid(s - 1):
-                square("prev", s - 1)
-            if SHARE and valid(s + 2):
-                slope(s - 1)
+            if s < last:
+                square("prev", s)
 
         store_y(last - 1)
-        for h in range(2):
-            stage2(last, h)
-        for h in range(2):
-            add_grad(last, h)
-        quant_y(last - 2)
-        store_planes(last - 2, [nc.sync] * 4)
+        both(stage2, last)
+        both(add_grad, last)
         turn_y(last - 1)
-        unload_y(last - 1)
         result(last, 0, BANK)
         store_y(last, 0, BANK)
         round_y(last, 0, nc.scalar.copy)
+        unload_y(last - 1)
         result(last, BANK, H)
         store_y(last, BANK, H)
         turn_y(last, (0,))
-        quant_y(last - 1, (0,))
+        quant_y(last - 2, (0,))
         round_y(last, 1, nc.vector.tensor_copy)
-        quant_y(last - 1, (1,))
+        quant_y(last - 2, (1,))
+        store_planes(last - 2, [nc.sync] * 4)
+        quant_y(last - 1)
         store_planes(last - 1, [nc.sync] * 4)
         unload_y(last, (0,))
         turn_y(last, (1,))

@@ -21,15 +21,15 @@ BANK = 512
 TILES = M // P
 CG = C // 512
 HG = H // 512
-E_CHUNKS = [(0, 1), (1, 3), (3, 6), (6, 9), (9, 12)]
-ES_CHUNKS = [(0, 3), (3, 12)]
-QUANT_CHUNKS = [(0, 2), (2, 4), (4, 6), (6, 8), (8, 9), (9, 10), (10, 11), (11, 12)]
-CODE_CHUNKS = [(0, 4), (4, 9), (9, 11), (11, 12)]
-SCALE_CHUNKS = [(0, 9), (9, 12)]
+E_CHUNKS = [(0, 1), (1, 3), (3, 5), (5, 8), (8, 12)]
+ES_CHUNKS = [(0, 4), (4, 12)]
+QUANT_CHUNKS = [(0, 2), (2, 4), (4, 6), (6, 8), (8, 10), (10, 11), (11, 12)]
+CODE_CHUNKS = [(0, 4), (4, 8), (8, 11), (11, 12)]
+SCALE_CHUNKS = [(0, 8), (8, 12)]
 LAG = 2
 RING = 6
 W_ON_V = 0
-CATCH = 9
+CATCH = 7
 SHARE = 0
 
 
@@ -271,94 +271,6 @@ def tile_rnn_step_backprop_h2_kernel(
             round_y(r, 1, gpsimd_copy)
             round_y(r, 0, nc.scalar.copy)
 
-        def deltas(s):
-            for h in range(2):
-                delta(s, h)
-
-        clear_plane(nc.vector, "es0", P * 3)
-        clear_plane(nc.vector, "hs0", BANK)
-        clear_plane(nc.vector, "hs1", BANK)
-        load_e(E_CHUNKS[0])
-        load_plane([nc.gpsimd, nc.gpsimd, nc.scalar, nc.scalar], "es0", e_scales, 0, P * 3)
-        load_plane([nc.scalar] * 4, "hs0", head_scales, 0, BANK)
-        load_head(0)
-        load_plane([nc.gpsimd] * 4, "hs1", head_scales, BANK, H)
-        ident = kept("ident", [P, P], F32)
-        make_identity(nc, ident[:])
-        clear_plane(nc.gpsimd, "es3", P * 9)
-        load_head(1)
-        load_rows("now", h_now, 0)
-        load_e(E_CHUNKS[1])
-        load_w(0)
-        load_rows("now", h_now, 1)
-        for pair in range(1, 4):
-            load_w(pair)
-        load_rows("now", h_now, 2)
-        load_rows("prev", h_prev, 0)
-        load_rows("grad", grad_prev, 0)
-        load_plane([nc.sync] * 4, "es3", e_scales, P * 3, M)
-        load_e(E_CHUNKS[2])
-        load_rows("prev", h_prev, 1)
-        load_rows("grad", grad_prev, 1)
-        load_rows("now", h_now, 3)
-        for s in range(2, 5):
-            if s < 4:
-                load_rows("now", h_now, s + 2)
-            load_rows("prev", h_prev, s)
-            load_rows("grad", grad_prev, s)
-
-        square("now", 0)
-        stage1(0)
-        deltas(0)
-        sort_w(0)
-        square("now", 1)
-        stage1(1, (0,))
-        turn_w(0)
-        turn_delta(0)
-        for n in range(HG):
-            unload_w(0, n)
-        sort_w(1)
-        delta(1, 0)
-        stage1(1, (1,))
-        turn_w(1)
-        unload_delta(0)
-        for n in range(HG):
-            unload_w(1, n)
-        delta(1, 1)
-        sort_w(2)
-        square("now", 2)
-        stage1(2, (0,))
-        turn_w(2)
-        turn_delta(1)
-        sort_w(3)
-        quant_delta(0)
-        for n in range(HG):
-            quant_w(0, n)
-        stage1(2, (1,))
-        turn_w(3)
-        for n in range(HG):
-            unload_w(2, n)
-        deltas(2)
-        unload_w(3, 0)
-        unload_w(3, 1, nc.vector.tensor_copy if W_ON_V & 2 else nc.scalar.copy)
-        unload_delta(1)
-        stage2(0, 0)
-        square("prev", 0)
-        add_grad(0, 0)
-        for n in range(HG):
-            quant_w(1, n)
-        square("now", 3)
-        result(0, 0, BANK)
-        quant_delta(1)
-        stage1(3)
-        stage2(0, 1)
-        square("prev", 1)
-        square("now", 4)
-        add_grad(0, 1)
-        deltas(3)
-        result(0, BANK, H)
-        finish(0)
-
         def loads(s):
             if valid(s + 3):
                 if s + 3 == chunk_of(E_CHUNKS, s + 3)[0]:
@@ -372,16 +284,117 @@ def tile_rnn_step_backprop_h2_kernel(
             for h in range(2):
                 f(r, h)
 
+        def deltas(s):
+            for h in range(2):
+                delta(s, h)
+
+        clear_plane(nc.vector, "es0", P * 4)
+        clear_plane(nc.vector, "hs0", BANK)
+        clear_plane(nc.vector, "hs1", BANK)
+        load_e(E_CHUNKS[0])
+        load_plane([nc.gpsimd, nc.gpsimd, nc.scalar, nc.scalar], "es0", e_scales, 0, P * 4)
+        load_plane([nc.scalar] * 4, "hs0", head_scales, 0, BANK)
+        load_head(0)
+        ident = kept("ident", [P, P], F32)
+        make_identity(nc, ident[:])
+        clear_plane(nc.gpsimd, "es4", P * 8)
+        load_rows("now", h_now, 0)
+        load_head(1)
+        load_plane([nc.scalar] * 4, "hs1", head_scales, BANK, H)
+        load_e(E_CHUNKS[1])
+        load_w(0)
+        load_rows("now", h_now, 1)
+        for pair in range(1, 4):
+            load_w(pair)
+        load_rows("now", h_now, 2)
+        load_rows("prev", h_prev, 0)
+        load_rows("grad", grad_prev, 0)
+        load_e(E_CHUNKS[2])
+        load_rows("now", h_now, 3)
+        load_rows("prev", h_prev, 1)
+        load_rows("grad", grad_prev, 1)
+        load_plane([nc.sync] * 4, "es4", e_scales, P * 4, M)
+        load_rows("now", h_now, 4)
+        load_rows("prev", h_prev, 2)
+        load_rows("grad", grad_prev, 2)
+        load_e(E_CHUNKS[3])
+        load_rows("now", h_now, 5)
+        for s in range(3, 5):
+            load_rows("prev", h_prev, s)
+            load_rows("grad", grad_prev, s)
+
+        square("now", 0)
+        stage1(0)
+        deltas(0)
+        sort_w(0)
+        square("now", 1)
+        stage1(1)
+        turn_w(0)
+        turn_delta(0)
+        for n in range(HG):
+            unload_w(0, n)
+        sort_w(1)
+        deltas(1)
+        unload_delta(0)
+        square("now", 2)
+        stage1(2, (0,))
+        turn_w(1)
+        turn_delta(1)
+        sort_w(2)
+        quant_delta(0)
+        sort_w(3)
+        for n in range(HG):
+            unload_w(1, n)
+        unload_delta(1)
+        delta(2, 0)
+        stage1(2, (1,))
+        for n in range(HG):
+            quant_w(0, n)
+        turn_w(2)
+        turn_w(3)
+        delta(2, 1)
+        stage2(0, 0)
+        for n in range(HG):
+            unload_w(2, n)
+            unload_w(3, n, nc.vector.tensor_copy if W_ON_V & (1 << n) else nc.scalar.copy)
+        square("now", 3)
+        square("prev", 0)
+        quant_delta(1)
+        add_grad(0, 0)
+        for n in range(HG):
+            quant_w(1, n)
+        stage1(3)
+        stage2(1, 0)
+        stage2(0, 1)
+        stage2(1, 1)
+        turn_delta(2)
+        delta(3, 0)
+        add_grad(0, 1)
+        delta(3, 1)
+        square("prev", 1)
+        unload_delta(2)
+        square("now", 4)
+        result(0)
+        quant_delta(2)
+        both(add_grad, 1)
+        finish(0)
+        square("now", 5)
+        square("prev", 2)
+        result(1, 0, BANK)
+        result(1, BANK, H)
+        finish(1)
+        loads(3)
+        store_y(0)
+
         last = TILES - 1
-        for s in range(3, CATCH):
+        for s in range(4, CATCH):
             r, b = s - 2, s - 4
             loads(s)
             store_y(r - 1)
             if valid(b - 2):
                 store_planes(b - 2, [nc.sync] * 4)
-            if s > 3:
-                stage1(s)
-                deltas(s)
+            stage1(s)
+            deltas(s)
             both(stage2, r)
             both(add_grad, r)
             turn_delta(s - 1)
@@ -434,7 +447,7 @@ def tile_rnn_step_backprop_h2_kernel(
 
         for s in range(CATCH + 1, TILES):
             r = s - 1
-            bs = [s - 3, s - 2] if s == CATCH + 1 else [s - 2]
+            bs = [s - 3, s - 2] if s == last else [s - 3]
             loads(s)
             stage1(s)
             delta(s, 0)
@@ -461,19 +474,17 @@ def tile_rnn_step_backprop_h2_kernel(
                 unload_delta(s)
             for b in bs[1:]:
                 unload_y(b)
-                quant_y(b - 1)
-                store_planes(b - 1, [nc.sync] * 4)
             result(r, 0, BANK)
             result(r, BANK, H)
             if s < last:
                 quant_delta(s)
-            if s == last:
-                square("prev", s)
             finish(r)
             if valid(s + 2):
                 square("now", s + 2)
             if s < last:
                 square("prev", s)
+            if s == last - 1:
+                square("prev", last)
 
         store_y(last - 1)
         both(stage2, last)
@@ -489,7 +500,6 @@ def tile_rnn_step_backprop_h2_kernel(
         quant_y(last - 2, (0,))
         round_y(last, 1, nc.vector.tensor_copy)
         quant_y(last - 2, (1,))
-        store_planes(last - 2, [nc.sync] * 4)
         quant_y(last - 1)
         store_planes(last - 1, [nc.sync] * 4)
         unload_y(last, (0,))

@@ -21,7 +21,7 @@ BANK = 512
 TILES = M // P
 CG = C // 512
 HG = H // 512
-E_CHUNKS = [(0, 1), (1, 3), (3, 5), (5, 8), (8, 12)]
+E_CHUNKS = [(0, 1), (1, 3), (3, 5), (5, 7), (7, 9), (9, 12)]
 ES_CHUNKS = [(0, 4), (4, 12)]
 QUANT_CHUNKS = [(0, 2), (2, 4), (4, 6), (6, 8), (8, 10), (10, 11), (11, 12)]
 CODE_CHUNKS = [(0, 4), (4, 8), (8, 11), (11, 12)]
@@ -29,8 +29,11 @@ SCALE_CHUNKS = [(0, 8), (8, 12)]
 LAG = 2
 RING = 6
 W_ON_V = 0
-CATCH = 7
-SHARE = 0
+CATCH = 9
+LATE_SQ = 0
+AHEAD = 1
+SHARE = 256
+SHARED = []
 
 
 def chunk_of(chunks, s):
@@ -70,20 +73,30 @@ def tile_rnn_step_backprop_h2_kernel(
             tile = kept("e%d" % lo, [P, CG, (hi - lo) * P], U32)
             nc.sync.dma_start(out=tile[:].bitcast(I32), in_=e_rows[:, :, 4 * P * lo : 4 * P * hi].bitcast(I32))
 
-        def clear_plane(eng, name, width):
-            plane = kept(name, [P, CG, width], U8)
+        def clear_plane(eng, plane):
             eng.memset(plane[:].bitcast(I32), 0)
 
-        def load_plane(queues, name, scales, lo, hi):
+        def load_plane(queues, plane, scales, lo, hi):
             for q in range(4):
                 queues[q].dma_start(
-                    out=t[name][q:P:32, :, :].bitcast(I32),
+                    out=plane[q:P:32, :, :].bitcast(I32),
                     in_=scales[:, q:16:4, lo:hi].rearrange("g r n -> r g n").bitcast(I32),
                 )
 
         def load_head(h):
-            tile = kept("head%d" % h, [P, CG, 2 * BANK], U8)
+            tile = rotating("y", ("head", h), [P, CG, 2 * BANK], U8, 4)
             nc.sync.dma_start(out=tile[:].bitcast(I32), in_=head_rows[:, :, 2 * BANK * h : 2 * BANK * (h + 1)].bitcast(I32))
+
+        def sort_bytes(name, src):
+            dst = kept(name, list(src.shape), U8)
+            nc.vector.tensor_copy(
+                out=dst[:].bitcast(I32).rearrange("p g (u q e) -> p g u q e", u=2, q=16),
+                in_=src[:].bitcast(I32).rearrange("p g (q u e) -> p g u q e", u=2, q=16),
+            )
+
+        def sort_head(h):
+            sort_bytes("head%d" % h, t["y", ("head", h)])
+            sort_bytes("hs%d" % h, t["total", ("hs", h)])
 
         def load_w(pair):
             tile = kept("w%d" % pair, [P, 2, H], BF16)
@@ -95,7 +108,14 @@ def tile_rnn_step_backprop_h2_kernel(
 
         def square(tag, s):
             sq = rotating("sq_" + tag, s, [P, H], F32, 3)
-            nc.scalar.activation(out=sq[:], in_=t[tag, s][:], func=ACT.Square)
+            if tag == "now":
+                nc.scalar.activation(
+                    out=sq[:].rearrange("p (u b e) -> p u b e", u=2, e=16),
+                    in_=t[tag, s][:].rearrange("p (b u e) -> p u b e", u=2, e=16),
+                    func=ACT.Square,
+                )
+            else:
+                nc.scalar.activation(out=sq[:], in_=t[tag, s][:], func=ACT.Square)
 
         def stage1(s, halves=(0, 1)):
             lo = chunk_of(E_CHUNKS, s)[0]
@@ -115,13 +135,14 @@ def tile_rnn_step_backprop_h2_kernel(
 
         def delta(s, h):
             dbf = rotating("dbf", (s, h), [P, BANK], BF16, 6)
-            sq = t["sq_now", s][:, BANK * h : BANK * (h + 1)].rearrange("p (q u e) -> p u q e", u=2, e=16)
-            acc = t["d", (s, h)][:].rearrange("p (q u e) -> p u q e", u=2, e=16)
-            dst = dbf[:].rearrange("p (u q e) -> p u q e", u=2, e=16)
-            for u in range(2):
-                nc.vector.scalar_tensor_tensor(
-                    out=dst[:, u], in0=sq[:, u], scalar=1.0, in1=acc[:, u], op0=ALU.subtract, op1=ALU.mult
-                )
+            nc.vector.scalar_tensor_tensor(
+                out=dbf[:].rearrange("p (u c) -> p u c", u=2),
+                in0=t["sq_now", s][:].rearrange("p (u h c) -> p h u c", u=2, h=2)[:, h],
+                scalar=1.0,
+                in1=t["d", (s, h)][:].rearrange("p (u c) -> p u c", u=2),
+                op0=ALU.subtract,
+                op1=ALU.mult,
+            )
 
         def turn(kind, key, sources):
             dst = bank(kind, key)
@@ -196,14 +217,17 @@ def tile_rnn_step_backprop_h2_kernel(
         def result(s, lo=0, hi=H):
             if ("y", s) not in t:
                 rotating("y", s, [P, H], F32, 4)
+            if s in SHARED:
+                hi = min(hi, H - SHARE)
             nc.vector.scalar_tensor_tensor(
                 out=t["y", s][:, lo:hi], in0=t["sq_prev", s][:, lo:hi], scalar=1.0, in1=t["total", s][:, lo:hi],
                 op0=ALU.subtract, op1=ALU.mult,
             )
 
         def slope(s):
-            dst = rotating("slope", s, [P, SHARE], F32, 3)
-            nc.scalar.activation(out=dst[:], in_=t["sq_prev", s][:, H - SHARE : H], func=ACT.Copy, bias=-1.0)
+            if s in SHARED:
+                dst = rotating("slope", s, [P, SHARE], F32, 3)
+                nc.scalar.activation(out=dst[:], in_=t["sq_prev", s][:, H - SHARE : H], func=ACT.Copy, bias=-1.0)
 
         def result_share(s):
             nc.gpsimd.tensor_tensor(
@@ -213,15 +237,15 @@ def tile_rnn_step_backprop_h2_kernel(
         def gpsimd_copy(out, in_):
             nc.gpsimd.tensor_scalar(out=out, in0=in_, scalar1=1.0, scalar2=0.0, op0=ALU.mult, op1=ALU.add)
 
-        def round_y(s, g, copy):
-            dst = rotating("ybf", (s, g), [P, BANK], BF16, 6)
-            copy(
-                out=dst[:].rearrange("p (u w e) -> p u w e", u=2, e=2),
-                in_=t["y", s][:, BANK * g : BANK * (g + 1)].rearrange("p (w u e) -> p u w e", u=2, e=2),
-            )
+        def round_y(s, g, copy, slots=(0, 1)):
+            dst = rotating("ybf%d" % len(slots), (s, g, slots), [P, len(slots), 2 * P], BF16, 6)
+            src = t["y", s][:, BANK * g : BANK * (g + 1)].rearrange("p (w u e) -> p u w e", u=2, e=2)
+            copy(out=dst[:].rearrange("p u (w e) -> p u w e", e=2), in_=src[:, slots[0] : slots[-1] + 1])
+            for k, u in enumerate(slots):
+                t["ybf", (s, g, u)] = dst[:, k, :].bitcast(F32)
 
         def turn_y(s, groups=(0, 1)):
-            turn("yT", (s, groups), [pairs(t["ybf", (s, g)], u) for g in groups for u in range(2)])
+            turn("yT", (s, groups), [t["ybf", (s, g, u)] for g in groups for u in range(2)])
 
         def unload_y(s, groups=(0, 1), copy=nc.scalar.copy):
             lo, hi = chunk_of(QUANT_CHUNKS, s)
@@ -268,17 +292,23 @@ def tile_rnn_step_backprop_h2_kernel(
             return 0 <= s < TILES
 
         def finish(r):
-            round_y(r, 1, gpsimd_copy)
-            round_y(r, 0, nc.scalar.copy)
+            if r in SHARED:
+                round_y(r, 0, gpsimd_copy, (1,))
+                result_share(r)
+                round_y(r, 1, gpsimd_copy)
+                round_y(r, 0, nc.scalar.copy, (0,))
+            else:
+                round_y(r, 1, gpsimd_copy)
+                round_y(r, 0, nc.scalar.copy)
 
         def loads(s):
             if valid(s + 3):
-                if s + 3 == chunk_of(E_CHUNKS, s + 3)[0]:
-                    load_e(chunk_of(E_CHUNKS, s + 3))
                 load_rows("now", h_now, s + 3)
-            if valid(s + 2):
-                load_rows("prev", h_prev, s + 2)
-                load_rows("grad", grad_prev, s + 2)
+            if valid(s + 2) and s + 2 == chunk_of(E_CHUNKS, s + 2)[0] > 5:
+                load_e(chunk_of(E_CHUNKS, s + 2))
+            if valid(s + AHEAD):
+                load_rows("prev", h_prev, s + AHEAD)
+                load_rows("grad", grad_prev, s + AHEAD)
 
         def both(f, r):
             for h in range(2):
@@ -288,19 +318,19 @@ def tile_rnn_step_backprop_h2_kernel(
             for h in range(2):
                 delta(s, h)
 
-        clear_plane(nc.vector, "es0", P * 4)
-        clear_plane(nc.vector, "hs0", BANK)
-        clear_plane(nc.vector, "hs1", BANK)
+        clear_plane(nc.vector, kept("es0", [P, CG, P * 4], U8))
+        for h in range(2):
+            clear_plane(nc.vector, rotating("total", ("hs", h), [P, CG, BANK], U8, 3))
         load_e(E_CHUNKS[0])
-        load_plane([nc.gpsimd, nc.gpsimd, nc.scalar, nc.scalar], "es0", e_scales, 0, P * 4)
-        load_plane([nc.scalar] * 4, "hs0", head_scales, 0, BANK)
+        load_plane([nc.gpsimd, nc.gpsimd, nc.scalar, nc.scalar], t["es0"], e_scales, 0, P * 4)
+        load_plane([nc.scalar] * 4, t["total", ("hs", 0)], head_scales, 0, BANK)
         load_head(0)
         ident = kept("ident", [P, P], F32)
         make_identity(nc, ident[:])
-        clear_plane(nc.gpsimd, "es4", P * 8)
+        clear_plane(nc.gpsimd, kept("es4", [P, CG, P * 8], U8))
         load_rows("now", h_now, 0)
         load_head(1)
-        load_plane([nc.scalar] * 4, "hs1", head_scales, BANK, H)
+        load_plane([nc.scalar] * 4, t["total", ("hs", 1)], head_scales, BANK, H)
         load_e(E_CHUNKS[1])
         load_w(0)
         load_rows("now", h_now, 1)
@@ -313,17 +343,19 @@ def tile_rnn_step_backprop_h2_kernel(
         load_rows("now", h_now, 3)
         load_rows("prev", h_prev, 1)
         load_rows("grad", grad_prev, 1)
-        load_plane([nc.sync] * 4, "es4", e_scales, P * 4, M)
+        load_plane([nc.sync] * 4, t["es4"], e_scales, P * 4, M)
         load_rows("now", h_now, 4)
         load_rows("prev", h_prev, 2)
         load_rows("grad", grad_prev, 2)
         load_e(E_CHUNKS[3])
         load_rows("now", h_now, 5)
-        for s in range(3, 5):
+        for s in range(3, 3 + AHEAD):
             load_rows("prev", h_prev, s)
             load_rows("grad", grad_prev, s)
 
         square("now", 0)
+        for h in range(2):
+            sort_head(h)
         stage1(0)
         deltas(0)
         sort_w(0)
@@ -336,7 +368,8 @@ def tile_rnn_step_backprop_h2_kernel(
         sort_w(1)
         deltas(1)
         unload_delta(0)
-        square("now", 2)
+        if not LATE_SQ:
+            square("now", 2)
         stage1(2, (0,))
         turn_w(1)
         turn_delta(1)
@@ -345,6 +378,8 @@ def tile_rnn_step_backprop_h2_kernel(
         sort_w(3)
         for n in range(HG):
             unload_w(1, n)
+        if LATE_SQ:
+            square("now", 2)
         unload_delta(1)
         delta(2, 0)
         stage1(2, (1,))
@@ -374,6 +409,7 @@ def tile_rnn_step_backprop_h2_kernel(
         square("prev", 1)
         unload_delta(2)
         square("now", 4)
+        slope(1)
         result(0)
         quant_delta(2)
         both(add_grad, 1)
@@ -383,6 +419,7 @@ def tile_rnn_step_backprop_h2_kernel(
         result(1, 0, BANK)
         result(1, BANK, H)
         finish(1)
+        slope(2)
         loads(3)
         store_y(0)
 
@@ -414,6 +451,7 @@ def tile_rnn_step_backprop_h2_kernel(
             quant_delta(s - 1)
             result(r)
             finish(r)
+            slope(r + 1)
 
         s = CATCH
         quant_delta(s - 1)
@@ -437,6 +475,7 @@ def tile_rnn_step_backprop_h2_kernel(
         result(s - 2)
         both(add_grad, s - 1)
         finish(s - 2)
+        slope(s - 1)
         square("now", s + 2)
         square("prev", s)
         quant_delta(s)
@@ -454,12 +493,12 @@ def tile_rnn_step_backprop_h2_kernel(
             if s == CATCH + 1:
                 result(s - 2)
                 finish(s - 2)
-            quant_y(bs[0] - 1)
             delta(s, 1)
             store_y(r - 1)
-            store_planes(bs[0] - 1, [nc.sync] * 4)
             both(stage2, r)
             both(add_grad, r)
+            quant_y(bs[0] - 1)
+            store_planes(bs[0] - 1, [nc.sync] * 4)
             if s == last:
                 for n in range(HG):
                     turn_delta(s, (n,))
@@ -470,6 +509,7 @@ def tile_rnn_step_backprop_h2_kernel(
             if s < last:
                 turn_delta(s)
             unload_y(bs[0])
+            slope(r)
             if s < last:
                 unload_delta(s)
             for b in bs[1:]:

from contextlib import ExitStack

import concourse.mybir as mybir
from concourse.masks import make_identity

M, C, H = 1536, 2048, 1024
FLOPS = 2 * M * C * H + 2 * M * H * H

F32 = mybir.dt.float32
BF16 = mybir.dt.bfloat16
I32 = mybir.dt.int32
U32 = mybir.dt.uint32
U8 = mybir.dt.uint8
FP8X4 = mybir.dt.float8_e4m3fn_x4
FP4X4 = mybir.dt.float4_e2m1fn_x4
ALU = mybir.AluOpType
ACT = mybir.ActivationFunctionType

P = 128
BANK = 512
TILES = M // P
CG = C // 512
HG = H // 512
E_CHUNKS = [(0, 1), (1, 3), (3, 5), (5, 7), (7, 9), (9, 12)]
ES_CHUNKS = [(0, 4), (4, 12)]
QUANT_CHUNKS = [(0, 2), (2, 4), (4, 6), (6, 8), (8, 10), (10, 11), (11, 12)]
CODE_CHUNKS = [(0, 4), (4, 8), (8, 11), (11, 12)]
SCALE_CHUNKS = [(0, 8), (8, 12)]
LAG = 2
RING = 6
W_ON_V = 0
CATCH = 9
LATE_SQ = 0
AHEAD = 1
SHARE = 256
SHARED = []


def chunk_of(chunks, s):
    return [c for c in chunks if c[0] <= s < c[1]][0]


def tile_rnn_step_backprop_h2_kernel(
    tc, e_words, e_scales, head_words, head_scales, w_rec, h_now, h_prev, grad_prev, out_0, out_1, out_2
):
    nc = tc.nc
    with ExitStack() as ctx:
        keep = ctx.enter_context(tc.tile_pool(name="keep", bufs=1))
        ring = ctx.enter_context(tc.tile_pool(name="ring", bufs=3))
        psum = ctx.enter_context(tc.psum_pool(name="psum", bufs=8))
        ctx.enter_context(tc.manual_schedule())

        t = {}

        def kept(name, shape, dtype):
            t[name] = keep.tile(shape, dtype, name=name, align_bytes=64)
            return t[name]

        def rotating(tag, key, shape, dtype, bufs):
            t[tag, key] = ring.tile(shape, dtype, name=tag, tag=tag, bufs=bufs, align_bytes=64)
            return t[tag, key]

        def bank(kind, key):
            t[kind, key] = psum.tile([P, BANK], F32, name="bank", tag="bank")
            return t[kind, key]

        e_rows = e_words.rearrange("g p m t -> p g (m t)")
        head_rows = head_words.rearrange("g p n -> p g n")
        code_rows = out_1.rearrange("g p m t -> p g (m t)")

        def load_e(c):
            lo, hi = c
            tile = kept("e%d" % lo, [P, CG, (hi - lo) * P], U32)
            nc.sync.dma_start(out=tile[:].bitcast(I32), in_=e_rows[:, :, 4 * P * lo : 4 * P * hi].bitcast(I32))

        def clear_plane(eng, plane):
            eng.memset(plane[:].bitcast(I32), 0)

        def load_plane(queues, plane, scales, lo, hi):
            for q in range(4):
                queues[q].dma_start(
                    out=plane[q:P:32, :, :].bitcast(I32),
                    in_=scales[:, q:16:4, lo:hi].rearrange("g r n -> r g n").bitcast(I32),
                )

        def load_head(h):
            tile = rotating("y", ("head", h), [P, CG, 2 * BANK], U8, 4)
            nc.sync.dma_start(out=tile[:].bitcast(I32), in_=head_rows[:, :, 2 * BANK * h : 2 * BANK * (h + 1)].bitcast(I32))

        def sort_bytes(name, src):
            dst = kept(name, list(src.shape), U8)
            nc.vector.tensor_copy(
                out=dst[:].bitcast(I32).rearrange("p g (u q e) -> p g u q e", u=2, q=16),
                in_=src[:].bitcast(I32).rearrange("p g (q u e) -> p g u q e", u=2, q=16),
            )

        def sort_head(h):
            sort_bytes("head%d" % h, t["y", ("head", h)])
            sort_bytes("hs%d" % h, t["total", ("hs", h)])

        def load_w(pair):
            tile = kept("w%d" % pair, [P, 2, H], BF16)
            nc.sync.dma_start(out=tile[:], in_=w_rec[2 * P * pair : 2 * P * (pair + 1), :].rearrange("(r p) j -> p r j", p=P))

        def load_rows(tag, src, s):
            tile = rotating(tag, s, [P, H], BF16, RING)
            nc.sync.dma_start(out=tile[:], in_=src[P * s : P * (s + 1), :])

        def square(tag, s):
            sq = rotating("sq_" + tag, s, [P, H], F32, 3)
            if tag == "now":
                nc.scalar.activation(
                    out=sq[:].rearrange("p (u b e) -> p u b e", u=2, e=16),
                    in_=t[tag, s][:].rearrange("p (b u e) -> p u b e", u=2, e=16),
                    func=ACT.Square,
                )
            else:
                nc.scalar.activation(out=sq[:], in_=t[tag, s][:], func=ACT.Square)

        def stage1(s, halves=(0, 1)):
            lo = chunk_of(E_CHUNKS, s)[0]
            slo = chunk_of(ES_CHUNKS, s)[0]
            for h, g in [(h, g) for h in halves for g in range(CG)]:
                if g == 0:
                    bank("d", (s, h))
                nc.tensor.matmul_mx(
                    out=t["d", (s, h)][:],
                    lhsT=t["e%d" % lo][:, g, P * (s - lo) : P * (s - lo + 1)].bitcast(FP8X4),
                    lhsT_scale=t["es%d" % slo][:, g, P * (s - slo) : P * (s - slo + 1)],
                    rhs=t["head%d" % h][:, g, :].bitcast(FP4X4),
                    rhs_scale=t["hs%d" % h][:, g, :],
                    start=(g == 0),
                    stop=(g == CG - 1),
                )

        def delta(s, h):
            dbf = rotating("dbf", (s, h), [P, BANK], BF16, 6)
            nc.vector.scalar_tensor_tensor(
                out=dbf[:].rearrange("p (u c) -> p u c", u=2),
                in0=t["sq_now", s][:].rearrange("p (u h c) -> p h u c", u=2, h=2)[:, h],
                scalar=1.0,
                in1=t["d", (s, h)][:].rearrange("p (u c) -> p u c", u=2),
                op0=ALU.subtract,
                op1=ALU.mult,
            )

        def turn(kind, key, sources):
            dst = bank(kind, key)
            for k, src in enumerate(sources):
                nc.tensor.transpose(dst[:, P * k : P * (k + 1)], src, t["ident"][:])

        def pairs(tile, k):
            return tile[:].bitcast(F32)[:, P * k : P * (k + 1)]

        def unload(kind, key, dst, n, copy=nc.scalar.copy):
            src = t[kind, key][:, 0 : 2 * P * n].rearrange("p (n u m) -> p n m u", u=2, m=P)
            copy(out=dst, in_=src)

        def turn_delta(s, passes=(0, 1)):
            turn("dT", (s, passes), [pairs(t["dbf", (s, n)], u) for n in passes for u in range(2)])

        def unload_delta(s, passes=(0, 1)):
            dst = rotating("dTs", (s, passes), [P, 2 * P * len(passes)], F32, 3)
            unload("dT", (s, passes), dst[:].rearrange("p (n m u) -> p n m u", u=2, m=P), len(passes))

        def quant_delta(s, passes=(0, 1)):
            if ("dq", s) not in t:
                rotating("dq", s, [P, HG * P], U32, 4)
                rotating("dsc", s, [P, HG * P], U8, 4)
            cols = slice(P * passes[0], P * (passes[-1] + 1))
            nc.vector.quantize_mx(
                out=t["dq", s][:, cols].bitcast(FP8X4), scales=t["dsc", s][:, cols], in_=t["dTs", (s, passes)][:].bitcast(BF16)
            )

        def sort_w(pair):
            dst = rotating("ws", pair, [P, 2 * H], BF16, 2)
            nc.vector.tensor_copy(
                out=dst[:].rearrange("p (n u q e) -> p n u q e", n=2 * HG, u=2, e=16),
                in_=t["w%d" % pair][:].rearrange("p r (n q u e) -> p (r n) u q e", n=HG, u=2, e=16),
            )

        def turn_w(pair):
            for n in range(HG):
                turn("wT", (pair, n), [pairs(t["ws", pair], 2 * HG * r + 2 * n + u) for r in range(2) for u in range(2)])

        def unload_w(pair, n, copy=nc.scalar.copy):
            h, half = divmod(pair, 2)
            if half == 0:
                kept("wT%d%d" % (h, n), [P, 2 * BANK], F32)
            dst = t["wT%d%d" % (h, n)][:, BANK * half : BANK * (half + 1)].rearrange("p (r m u) -> p r m u", u=2, m=P)
            unload("wT", (pair, n), dst, 2, copy)

        def quant_w(h, n):
            codes = kept("wq%d%d" % (h, n), [P, BANK], U32)
            scales = kept("wsc%d%d" % (h, n), [P, BANK], U8)
            nc.vector.quantize_mx(out=codes[:].bitcast(FP8X4), scales=scales[:], in_=t["wT%d%d" % (h, n)][:].bitcast(BF16))

        def stage2(s, h):
            acc = bank("r", (s, h))
            for n in range(HG):
                nc.tensor.matmul_mx(
                    out=acc[:],
                    lhsT=t["dq", s][:, P * n : P * (n + 1)].bitcast(FP8X4),
                    lhsT_scale=t["dsc", s][:, P * n : P * (n + 1)],
                    rhs=t["wq%d%d" % (h, n)][:].bitcast(FP8X4),
                    rhs_scale=t["wsc%d%d" % (h, n)][:],
                    start=(n == 0),
                    stop=(n == HG - 1),
                )

        def add_grad(s, h):
            if ("total", s) not in t:
                rotating("total", s, [P, H], F32, 3)
            cols = slice(BANK * h, BANK * (h + 1))
            nc.vector.tensor_tensor(out=t["total", s][:, cols], in0=t["r", (s, h)][:], in1=t["grad", s][:, cols], op=ALU.subtract)

        def result(s, lo=0, hi=H):
            if ("y", s) not in t:
                rotating("y", s, [P, H], F32, 4)
            if s in SHARED:
                hi = min(hi, H - SHARE)
            nc.vector.scalar_tensor_tensor(
                out=t["y", s][:, lo:hi], in0=t["sq_prev", s][:, lo:hi], scalar=1.0, in1=t["total", s][:, lo:hi],
                op0=ALU.subtract, op1=ALU.mult,
            )

        def slope(s):
            if s in SHARED:
                dst = rotating("slope", s, [P, SHARE], F32, 3)
                nc.scalar.activation(out=dst[:], in_=t["sq_prev", s][:, H - SHARE : H], func=ACT.Copy, bias=-1.0)

        def result_share(s):
            nc.gpsimd.tensor_tensor(
                out=t["y", s][:, H - SHARE : H], in0=t["slope", s][:], in1=t["total", s][:, H - SHARE : H], op=ALU.mult
            )

        def gpsimd_copy(out, in_):
            nc.gpsimd.tensor_scalar(out=out, in0=in_, scalar1=1.0, scalar2=0.0, op0=ALU.mult, op1=ALU.add)

        def round_y(s, g, copy, slots=(0, 1)):
            dst = rotating("ybf%d" % len(slots), (s, g, slots), [P, len(slots), 2 * P], BF16, 6)
            src = t["y", s][:, BANK * g : BANK * (g + 1)].rearrange("p (w u e) -> p u w e", u=2, e=2)
            copy(out=dst[:].rearrange("p u (w e) -> p u w e", e=2), in_=src[:, slots[0] : slots[-1] + 1])
            for k, u in enumerate(slots):
                t["ybf", (s, g, u)] = dst[:, k, :].bitcast(F32)

        def turn_y(s, groups=(0, 1)):
            turn("yT", (s, groups), [t["ybf", (s, g, u)] for g in groups for u in range(2)])

        def unload_y(s, groups=(0, 1), copy=nc.scalar.copy):
            lo, hi = chunk_of(QUANT_CHUNKS, s)
            if ("yTs", lo) not in t:
                rotating("yTs", lo, [P, HG, 4 * P], F32, 3)
            dst = t["yTs", lo][:, groups[0] : groups[-1] + 1, 2 * P * (s - lo) : 2 * P * (s - lo + 1)]
            unload("yT", (s, groups), dst.rearrange("p n (m u) -> p n m u", u=2), len(groups), copy)

        def quant_y(s, groups=(0, 1)):
            first, end = chunk_of(QUANT_CHUNKS, s)
            if s != end - 1:
                return
            lo, hi = chunk_of(CODE_CHUNKS, s)
            slo, shi = chunk_of(SCALE_CHUNKS, s)
            if "yq%d" % lo not in t:
                kept("yq%d" % lo, [P, HG, P * (hi - lo)], U32)
            if "ysc%d" % slo not in t:
                kept("ysc%d" % slo, [P, HG, P * (shi - slo)], U8)
            for g in groups:
                nc.vector.quantize_mx(
                    out=t["yq%d" % lo][:, g, P * (first - lo) : P * (end - lo)].bitcast(FP8X4),
                    scales=t["ysc%d" % slo][:, g, P * (first - slo) : P * (end - slo)],
                    in_=t["yTs", first][:, g, 0 : 2 * P * (end - first)].bitcast(BF16),
                )

        def store_y(s, lo=0, hi=H):
            nc.sync.dma_start(out=out_0[P * s : P * (s + 1), lo:hi], in_=t["y", s][:, lo:hi])

        def store_planes(s, queues):
            lo, hi = chunk_of(CODE_CHUNKS, s)
            if s == hi - 1:
                nc.sync.dma_start(
                    out=code_rows[:, :, 4 * P * lo : 4 * P * hi].bitcast(I32), in_=t["yq%d" % lo][:].bitcast(I32)
                )
            lo, hi = chunk_of(SCALE_CHUNKS, s)
            if s == hi - 1:
                for q in range(4):
                    queues[q].dma_start(
                        out=out_2[:, 4 * q : 4 * q + 4, P * lo : P * hi].rearrange("g r m -> r g m").bitcast(I32),
                        in_=t["ysc%d" % lo][32 * q : 32 * q + 4, :, :].bitcast(I32),
                    )

        def valid(s):
            return 0 <= s < TILES

        def finish(r):
            if r in SHARED:
                round_y(r, 0, gpsimd_copy, (1,))
                result_share(r)
                round_y(r, 1, gpsimd_copy)
                round_y(r, 0, nc.scalar.copy, (0,))
            else:
                round_y(r, 1, gpsimd_copy)
                round_y(r, 0, nc.scalar.copy)

        def loads(s):
            if valid(s + 3):
                load_rows("now", h_now, s + 3)
            if valid(s + 2) and s + 2 == chunk_of(E_CHUNKS, s + 2)[0] > 5:
                load_e(chunk_of(E_CHUNKS, s + 2))
            if valid(s + AHEAD):
                load_rows("prev", h_prev, s + AHEAD)
                load_rows("grad", grad_prev, s + AHEAD)

        def both(f, r):
            for h in range(2):
                f(r, h)

        def deltas(s):
            for h in range(2):
                delta(s, h)

        clear_plane(nc.vector, kept("es0", [P, CG, P * 4], U8))
        for h in range(2):
            clear_plane(nc.vector, rotating("total", ("hs", h), [P, CG, BANK], U8, 3))
        load_e(E_CHUNKS[0])
        load_plane([nc.gpsimd, nc.gpsimd, nc.scalar, nc.scalar], t["es0"], e_scales, 0, P * 4)
        load_plane([nc.scalar] * 4, t["total", ("hs", 0)], head_scales, 0, BANK)
        load_head(0)
        ident = kept("ident", [P, P], F32)
        make_identity(nc, ident[:])
        clear_plane(nc.gpsimd, kept("es4", [P, CG, P * 8], U8))
        load_rows("now", h_now, 0)
        load_head(1)
        load_plane([nc.scalar] * 4, t["total", ("hs", 1)], head_scales, BANK, H)
        load_e(E_CHUNKS[1])
        load_w(0)
        load_rows("now", h_now, 1)
        for pair in range(1, 4):
            load_w(pair)
        load_rows("now", h_now, 2)
        load_rows("prev", h_prev, 0)
        load_rows("grad", grad_prev, 0)
        load_e(E_CHUNKS[2])
        load_rows("now", h_now, 3)
        load_rows("prev", h_prev, 1)
        load_rows("grad", grad_prev, 1)
        load_plane([nc.sync] * 4, t["es4"], e_scales, P * 4, M)
        load_rows("now", h_now, 4)
        load_rows("prev", h_prev, 2)
        load_rows("grad", grad_prev, 2)
        load_e(E_CHUNKS[3])
        load_rows("now", h_now, 5)
        for s in range(3, 3 + AHEAD):
            load_rows("prev", h_prev, s)
            load_rows("grad", grad_prev, s)

        square("now", 0)
        for h in range(2):
            sort_head(h)
        stage1(0)
        deltas(0)
        sort_w(0)
        square("now", 1)
        stage1(1)
        turn_w(0)
        turn_delta(0)
        for n in range(HG):
            unload_w(0, n)
        sort_w(1)
        deltas(1)
        unload_delta(0)
        if not LATE_SQ:
            square("now", 2)
        stage1(2, (0,))
        turn_w(1)
        turn_delta(1)
        sort_w(2)
        quant_delta(0)
        sort_w(3)
        for n in range(HG):
            unload_w(1, n)
        if LATE_SQ:
            square("now", 2)
        unload_delta(1)
        delta(2, 0)
        stage1(2, (1,))
        for n in range(HG):
            quant_w(0, n)
        turn_w(2)
        turn_w(3)
        delta(2, 1)
        stage2(0, 0)
        for n in range(HG):
            unload_w(2, n)
            unload_w(3, n, nc.vector.tensor_copy if W_ON_V & (1 << n) else nc.scalar.copy)
        square("now", 3)
        square("prev", 0)
        quant_delta(1)
        add_grad(0, 0)
        for n in range(HG):
            quant_w(1, n)
        stage1(3)
        stage2(1, 0)
        stage2(0, 1)
        stage2(1, 1)
        turn_delta(2)
        delta(3, 0)
        add_grad(0, 1)
        delta(3, 1)
        square("prev", 1)
        unload_delta(2)
        square("now", 4)
        slope(1)
        result(0)
        quant_delta(2)
        both(add_grad, 1)
        finish(0)
        square("now", 5)
        square("prev", 2)
        result(1, 0, BANK)
        result(1, BANK, H)
        finish(1)
        slope(2)
        loads(3)
        store_y(0)

        last = TILES - 1
        for s in range(4, CATCH):
            r, b = s - 2, s - 4
            loads(s)
            store_y(r - 1)
            if valid(b - 2):
                store_planes(b - 2, [nc.sync] * 4)
            stage1(s)
            deltas(s)
            both(stage2, r)
            both(add_grad, r)
            turn_delta(s - 1)
            if valid(b):
                turn_y(b)
            if s == CATCH - 1:
                turn_delta(s)
            unload_delta(s - 1)
            if valid(b):
                unload_y(b)
            if s == CATCH - 1:
                unload_delta(s)
            square("now", s + 2)
            square("prev", r + 1)
            if valid(b - 1):
                quant_y(b - 1)
            quant_delta(s - 1)
            result(r)
            finish(r)
            slope(r + 1)

        s = CATCH
        quant_delta(s - 1)
        loads(s)
        store_y(s - 3)
        if valid(s - 6):
            store_planes(s - 6, [nc.sync] * 4)
        square("prev", s - 1)
        stage1(s)
        deltas(s)
        both(stage2, s - 2)
        both(stage2, s - 1)
        both(add_grad, s - 2)
        turn_y(s - 4)
        turn_delta(s)
        turn_y(s - 3)
        unload_y(s - 4)
        unload_delta(s)
        unload_y(s - 3)
        quant_y(s - 5)
        result(s - 2)
        both(add_grad, s - 1)
        finish(s - 2)
        slope(s - 1)
        square("now", s + 2)
        square("prev", s)
        quant_delta(s)
        quant_y(s - 4)
        store_y(s - 2)
        for b in (s - 5, s - 4):
            store_planes(b, [nc.sync] * 4)

        for s in range(CATCH + 1, TILES):
            r = s - 1
            bs = [s - 3, s - 2] if s == last else [s - 3]
            loads(s)
            stage1(s)
            delta(s, 0)
            if s == CATCH + 1:
                result(s - 2)
                finish(s - 2)
            delta(s, 1)
            store_y(r - 1)
            both(stage2, r)
            both(add_grad, r)
            quant_y(bs[0] - 1)
            store_planes(bs[0] - 1, [nc.sync] * 4)
            if s == last:
                for n in range(HG):
                    turn_delta(s, (n,))
                    unload_delta(s, (n,))
                    quant_delta(s, (n,))
            for b in bs:
                turn_y(b)
            if s < last:
                turn_delta(s)
            unload_y(bs[0])
            slope(r)
            if s < last:
                unload_delta(s)
            for b in bs[1:]:
                unload_y(b)
            result(r, 0, BANK)
            result(r, BANK, H)
            if s < last:
                quant_delta(s)
            finish(r)
            if valid(s + 2):
                square("now", s + 2)
            if s < last:
                square("prev", s)
            if s == last - 1:
                square("prev", last)

        store_y(last - 1)
        both(stage2, last)
        both(add_grad, last)
        turn_y(last - 1)
        result(last, 0, BANK)
        store_y(last, 0, BANK)
        round_y(last, 0, nc.scalar.copy)
        unload_y(last - 1)
        result(last, BANK, H)
        store_y(last, BANK, H)
        turn_y(last, (0,))
        quant_y(last - 2, (0,))
        round_y(last, 1, nc.vector.tensor_copy)
        quant_y(last - 2, (1,))
        quant_y(last - 1)
        store_planes(last - 1, [nc.sync] * 4)
        unload_y(last, (0,))
        turn_y(last, (1,))
        unload_y(last, (1,))
        quant_y(last)
        store_planes(last, [nc.scalar, nc.sync, nc.scalar, nc.sync])
